import numpy as np, ml_dtypes
CORES = [6,15,38,47]
N = 4
import mx_ref
BF = ml_dtypes.bfloat16
def gcols(t, e):
    v = np.concatenate([t.reshape(8, 16, -1, 4), np.zeros((8, 16, 1, 4), BF)], axis=2)
    return np.ascontiguousarray(np.stack([v[g][:, e[g]] for g in range(8)])).reshape(128, -1)
def tile(rs):
    return np.stack(rs, axis=2).reshape(128, -1).astype(BF)
def pick(q, e):
    c = np.concatenate([q[0].reshape(128, -1, 4), np.zeros((128, 1, 4), np.uint8)], axis=1); s = np.concatenate([q[1], np.ones((16, 1), np.uint8)], axis=1)
    return (np.ascontiguousarray(c[:, e].reshape(128, -1)), np.ascontiguousarray(s[:, e]))
def join(*qs):
    return (np.concatenate([q[0] for q in qs], axis=1), np.concatenate([q[1] for q in qs], axis=1))
def put(q, e, v):
    c, s = q[0].reshape(128, -1, 4).copy(), q[1].copy(); c[:, e] = v[0].reshape(128, -1, 4); s[:, e] = v[1]
    return (c.reshape(128, -1), s)
def pk(c, s):
    return (np.ascontiguousarray(c), mx_ref.live(s))
def emit(q):
    return q[0], q[1]
def packed(v, rng):
    q = [mx_ref.quantize(np.ascontiguousarray(v[r])) for r in range(N)]
    return np.stack([a for a, b in q]), np.stack([mx_ref.plane(b, rng) for a, b in q])
def values_of_codes():
    e, c = np.zeros((128, 128, 4), np.float32), np.zeros((128, 2, 4), np.uint8)
    e[np.arange(128), np.arange(128), 0] = 1
    c[:127, :, 0] = np.arange(256).reshape(2, 128).T[:127]
    return mx_ref.matmul(mx_ref.quantize(e.reshape(128, 512).astype(BF)), (c.reshape(128, 8), np.full((16, 2), 127, np.uint8))).T.reshape(-1).astype(np.float64)
CODE_VALUE, SCALE_VALUE = values_of_codes(), 2.0 ** (np.arange(256) - 127.0)
def decode(q):
    return (CODE_VALUE[q[0]].reshape(16, 8, -1, 4) * SCALE_VALUE[q[1]][:, None, :, None] + 0.0).reshape(128, -1).astype(np.float32)
def f(rng, *shape):
    return mx_ref.flush((rng.standard_normal(shape, dtype=np.float32) * np.exp2(rng.integers(-2, 3, shape[:-1] + (1,)))).astype(BF))
def wide(rng, *shape, cols=0):
    v = rng.standard_normal(shape, dtype=np.float32) * np.exp2(rng.integers(-12, 13, shape)).astype(np.float32)
    if cols: v *= np.repeat(np.exp2(rng.integers(-cols, cols + 1, shape[:-2] + (1, shape[-1] // 4))) * (rng.random(shape[:-2] + (1, shape[-1] // 4)) > 0.0625), 4, axis=-1).astype(np.float32)
    return mx_ref.flush(v.astype(BF))
C, M, R = 384, 40, 3
def numbers_of(rng):
    return {"x": np.array(f(rng, N, 128, 4 * C)), "u": np.array(f(rng, N, 128, 512)), "v": np.array(f(rng, N, 128, 512))}
def weights(rng, still=0):
    w = np.array(f(rng, N, 128, 2048)).reshape(N, 8, 16, 4, 8, 16, 4)
    w[:, :, :still] = 0
    w[:, :, :, :, :, :still] = 0
    c, p = packed(np.ascontiguousarray(w).reshape(N, 128, 2048), rng)
    return {"wc": c, "ws": p}
def plant(rng, d, word, sym, size, full=False):
    x, u = d["x"].reshape(N, 8, 16, C, 4), d["u"].reshape(N, 8, 16, 128, 4)
    low = rng.integers(-1, 1, (N, 8, 3))
    size = np.reshape(size, (N, 1, 1, 1))
    x[:, :, :8] = 0
    for k in range(3): u[:, :, :, k::16] = 0
    for g in range(8):
        h = (g + 1) % 8
        s = np.take_along_axis(sym[:, g], word & ~(1 << h), axis=1)
        for k, yes in enumerate((word >> g, s >> 1, s)):
            i, j, m = ((0, 6, 4), (6, 7, 4), (7, 8, 4))[k] if full else (k, k + 1, 1)
            a = np.where(yes & 1, 1, low[:, g, k, None])[:, None, :, None] * size
            x[:, h, i:j, :, :m] = a.astype(np.float32).astype(BF)
            u[:, h, i:j, 16 * g + k, :m] = size[:, :, :, 0].astype(np.float32).astype(BF)
def setup_inputs(rng):
    return {**numbers_of(rng), **weights(rng)}
def setup_inputs_caps(rng):
    d = numbers_of(rng)
    w = np.concatenate([np.repeat(np.arange(8), [M, M + 1, M, M - 1, 2 * M, 1, 0, 0]), np.full(C - 6 * M - 1, 8)])
    word = np.stack([(255 - (1 << np.append(rng.permutation(8), 8)) % 256)[rng.permutation(w)] for r in range(N)])
    sym = rng.integers(0, 4, (N, 8, 256))
    for g in range(8):
        h = (g + 1) % 8
        sym[:, g, 255 - (1 << h)] = rng.integers(4)
        sym[:, g, 255 - (1 << h) - (1 << g)] = sym[0, g, 255 - (1 << h)]
    plant(rng, d, word, sym, np.ones(N))
    return {**d, **weights(rng, 8)}
def setup_inputs_near(rng):
    d = numbers_of(rng)
    o = rng.permutation(N) % 2
    word = rng.integers(0, 256, (N, C))
    word[:, 0] = 255
    j = rng.integers(1, C, N)
    word[np.arange(N), j] = 255
    sym = rng.integers(0, 4, (N, 8, 256))
    sym[rng.integers(N)] = rng.integers(0, 4, (8, 1))
    plant(rng, d, word, sym, np.where(o == 0, 2.0 ** -30, 1.0))
    x = d["x"].reshape(N, 8, 16, C, 4)
    for r in range(N):
        for h in rng.permutation(8)[:4]: x[r, h, :3, j[r]] = (x[r, h, :3, j[r]].astype(np.float32) * np.float32(2.0 ** 50 if o[r] == 0 else 2.0 ** 20)).astype(BF)
    return {**d, **weights(rng, 8)}
def setup_inputs_huge(rng):
    d = numbers_of(rng)
    sym = rng.integers(0, 4, (N, 8, 256))
    g, none = int(rng.integers(8)), int(rng.integers(N))
    word = np.zeros((N, C), np.int64)
    for r in range(N):
        word[r] = rng.integers(256)
        if r == none: continue
        o = (g + 2 + rng.permutation(6)) % 8
        k = rng.integers(0, 16, C)
        k[:8] = 2 * np.arange(8) + 1
        k[8:8 + 4 * M] = 2 * (np.arange(4 * M) // M) + 8 * rng.integers(0, 2, 4 * M)
        k = rng.permutation(k)
        for i, e in enumerate((g, int(o[0]), int(o[1]), int(rng.choice(np.append(o[2:], (g + 1) % 8))))):
            word[r] = word[r] & ~(1 << e) | ((k >> i) & 1) << e
        n = np.arange(256)
        sym[r, g] = (2 * ((n >> int(o[1])) & 1) + ((n >> int(o[0])) & 1)) ^ int(rng.integers(4))
    d["x"] = (d["x"].astype(np.float32) * np.float32(2.0 ** 20)).astype(BF)
    plant(rng, d, word, sym, np.full(N, 2.0 ** 30), True)
    return {**d, **weights(rng, 8)}
def setup_inputs_late(rng):
    d = numbers_of(rng)
    x, u = d["x"].reshape(N, 8, 16, C, 4), d["u"].reshape(N, 128, 128, 4)
    k = (N, 8, 8, C, 4)
    a = np.exp2(-rng.integers(8, 15, k).astype(np.float64)) * (1.0 + (2 * rng.integers(0, 64, k) + 1) * 2.0 ** -7) * rng.choice([-1.0, 1.0], k)
    a[:, :, 0, :, 0] = 1.96875 * rng.choice([-1.0, 1.0], (N, 8, C))
    a[:, :, 1:4, :, 0] = 2.0 ** -13
    a[:, :, 4:7, :, 0] = 7 * 2.0 ** -16
    x[:, :, 8:] = a.astype(np.float32).astype(BF)
    x[:, :, :3, :, 0] = -0.0625
    for r in range(N):
        g = rng.permutation(C) % 16
        j = np.flatnonzero(g < 8)
        x[r, g[j], :3, j, 0] = 0
    s = (rng.permutation(N) % 2 * 2.0 - 1.0).astype(np.float32).astype(BF)
    for i in range(3):
        u[:, :, i::16] = 0
        for h in range(i, 128, 16):
            u[:, h, h, 0] = s
            u[:, h + 9, h, 0] = -s
            u[:, h + 12, h, 0] = s
    return {**d, **weights(rng)}
def setup_inputs_spread(rng):
    d = setup_inputs(rng)
    d["x"] = wide(rng, N, 128, 4 * C, cols=6)
    return d
def check_inputs(d):
    b = []
    for k in ("x", "u", "v"):
        a = np.abs(d[k].astype(np.float32))
        if not (np.isfinite(a).all() and ((a == 0) | (a >= 2.0 ** -30) & (a <= 2.0 ** 30)).all()): b.append("a value of " + k)
    none, least, most = [emit(mx_ref.quantize(np.full((128, 16), k, np.float32).astype(BF)))[1][0, 0] for k in (0.0, 2.0 ** -30, 2.0 ** 30)]
    for r in range(N):
        if ((d["wc"][r] == 0x7F) | (d["wc"][r] == 0xFF)).any(): b.append("wc: a code that is no number")
        s = mx_ref.live(d["ws"][r])
        if ((s != none) & ((s < least) | (s > most))).any(): b.append("ws: a scale out of range")
    return b
def mine(s):
    bit = s[::16] > 0
    word = np.packbits(bit, axis=0, bitorder="little")[0].astype(np.int64)
    sym = 2 * (s[1::16] > 0) + (s[2::16] > 0)
    first = np.full(256, -1)
    k, i = np.unique(word, return_index=True)
    first[k] = i
    a, b, take = np.full((8, 4 * M), -1), np.full((8, 4 * M), -1), np.zeros((8, C), np.int64)
    for g in range(8):
        mate = first[word ^ (1 << g)]
        for c in range(4):
            j = np.flatnonzero(~bit[g] & (mate >= 0) & (sym[g] == c))[:M]
            a[g, M * c:M * c + len(j)] = j
            b[g, M * c:M * c + len(j)] = mate[j]
            i = np.flatnonzero(sym[g] == c)
            take[g, i] = M * c + np.arange(len(i)) % M
    return a, b, take
def reference(x, u, v, wc, ws):
    qu = [mx_ref.quantize(u[r]) for r in range(N)]
    lay = [pk(wc[r], ws[r]) for r in range(N)]
    now = [x[r] for r in range(N)]
    for t in range(R):
        own, sent, takes = [], [], []
        for r in range(N):
            q = mx_ref.quantize(now[r])
            own.append(decode(q).astype(BF))
            a, b, take = mine(mx_ref.matmul(qu[r], q))
            e = (gcols(own[r], b).astype(np.float32) - gcols(own[r], a).astype(np.float32)).astype(BF)
            sent.append(mx_ref.quantize(e))
            takes.append(take)
        for r in range(N):
            came = decode(sent[(r - 1 - t) % N]).astype(BF)
            z = (own[r].astype(np.float32) + gcols(came, takes[r]).astype(np.float32)).astype(BF)
            q = mx_ref.quantize(z)
            now[r] = tile([np.maximum(mx_ref.matmul(pick(lay[r], np.arange(128 * b, 128 * b + 128)), q), np.float32(0.0)) * np.float32(0.015625) + z[:, b::4].astype(np.float32) for b in range(4)])
    y = np.zeros((N, 128, C), np.float32)
    oc, osc = np.zeros((N, 128, 4 * C), np.uint8), np.zeros((N, 16, C), np.uint8)
    for r in range(N):
        q = mx_ref.quantize(now[r])
        y[r] = mx_ref.matmul(mx_ref.quantize(v[r]), q)
        oc[r], osc[r] = emit(q)
    return {"y": y, "oc": oc, "osc": osc}

@@ -1,0 +1,473 @@
+from concourse.mybir import dt, AluOpType as A, AxisListType, ActivationFunctionType as AF
+
+N, C, R, NS = 4, 384, 3, 160
+H = C // 2
+CP = C + 32
+STEP = 1024.0
+BIG = float(2 ** 30)
+MAGIC = 1.5 * 2 ** 23
+DUMP = 1600
+SLOT0 = 2048 - DUMP
+F32, BF, I32, U16, CO, SC = "float32", "bfloat16", "int32", "uint16", "float8_e4m3fn_x4", "uint8"
+
+
+def _s(n, d):
+    return ("sbuf", [128, n], d)
+
+
+SCRATCH = {
+    "ps": ("psum", [128, 4096], F32),
+    "x0": _s(4 * C, BF), "ub": _s(512, BF), "vb": _s(512, BF),
+    "wq": _s(512, CO), "wz": _s(512, SC), "uq": _s(128, CO), "uz": _s(128, SC), "vq": _s(128, CO), "vz": _s(128, SC),
+    "et": _s(528, BF), "eq": _s(512, CO), "ez": _s(512, SC),
+    "ct": _s(1536, BF), "cq": _s(384, CO), "cz": _s(384, SC),
+    "xs": _s(4 * C, BF), "xq": _s(C, CO), "xz": _s(C, SC),
+    "zt": _s(4 * C, BF), "zq": _s(C, CO), "zz": _s(C, SC),
+    "bt": _s(4 * CP, BF), "bq": _s(CP, CO), "bz": _s(CP, SC),
+    "it": _s(512, BF), "iq": _s(128, CO), "iz": _s(128, SC),
+    "ff": _s(4 * C, BF), "nf": _s(4 * C, BF), "gg": _s(4 * NS, BF), "ga": _s(4 * C, BF), "aa": _s(4 * NS, BF),
+    "ee": _s(4 * NS, BF), "rr": _s(4 * C, F32), "yy": _s(C, F32),
+    "hb": _s(448, F32), "tab": _s(512, F32), "dk": _s(C, F32), "mp": _s(C, F32), "dm": _s(C + 16, BF), "sn": _s(C, BF),
+    "win": _s(1984, F32), "de": _s(NS, F32),
+    "key": _s(24, U16), "keyf": _s(24, F32), "fr": _s(24, F32), "thr": _s(128, F32),
+    "inc": _s(128, F32), "bb": _s(128, F32), "sm": _s(128, F32),
+    "pos": _s(24, U16), "a16": _s(10, U16), "pi": _s(10, I32), "pb": _s(10, I32), "b16": _s(10, U16),
+    "tq": _s(24, I32), "tr": _s(24, F32), "tv": _s(24, F32), "tk": _s(24, U16),
+    "cs": _s(64, F32), "p2": _s(1, F32), "k16": _s(16, F32), "hf": _s(8, F32), "z8": _s(8, F32), "v8": _s(8, F32),
+    "fi": _s(8, I32), "fl": _s(8, F32), "t8": _s(8, F32), "m3c": _s(4, F32), "ini": _s(2, F32), "ko": _s(4, F32),
+    "tg": _s(4, F32), "q2": _s(128, F32), "nm": _s(128, F32), "n2": _s(128, F32), "nb": _s(128, BF),
+    "d0a": _s(16, F32), "d0b": _s(16, F32), "lr": _s(24, U16), "d0": _s(C, BF), "d2b": _s(16, F32), "d2": _s(C, BF),
+    "ji": _s(C, F32), "jc": _s(C, F32), "d1": _s(2 * CP, BF),
+    "ig": _s(128, F32), "g4": _s(128, F32), "ua": _s(128, F32), "ios": _s(120, F32), "d1r": _s(120, F32),
+    "big": _s(24, F32), "idp": _s(24, F32), "ik": _s(8, F32), "ci": _s(8, I32), "l2": _s(8, U16),
+}
+for _t in range(R):
+    SCRATCH["oq%d" % _t] = _s(NS, CO)
+    SCRATCH["oz%d" % _t] = _s(NS, SC)
+    SCRATCH["lq%d" % _t] = _s(NS, CO)
+    SCRATCH["lz%d" % _t] = _s(NS, SC)
+
+SEMAPHORES = ["v", "a", "p", "g", "lx0", "lx1", "lu", "lv", "lwc", "lws", "arr0", "arr1", "arr2", "snt",
+              "st_sy", "st_sc"]
+
+
+def rank_program(g, core, T, topo):
+    rank = T.rank_of(core)
+    if rank is None:
+        return
+    Q = {"v": g.vector, "a": g.scalar, "p": g.tensor, "g": g, "sy": g.sync}
+    known = {q: {} for q in Q}
+    count = {}
+    snap = {}
+    wrote = {}
+    read = {}
+
+    def need(q, mark):
+        sem, val = mark
+        if known[q].get(sem, 0) >= val:
+            return
+        Q[q].wait_ge(T.sem[sem], val)
+        for s, x in snap.get(mark, {}).items():
+            if known[q].get(s, 0) < x:
+                known[q][s] = x
+        known[q][sem] = val
+
+    def op(q, fn, rd, wr, sem=None, inc=1):
+        sem = sem or q
+        marks = {}
+
+        def add(m, same):
+            if m is None or (m[0] == q and (q == "p" or not same)):
+                return
+            if marks.get(m[0], 0) < m[1]:
+                marks[m[0]] = m[1]
+        for k in rd:
+            add(wrote.get(k), True)
+            if k[0] == "#":
+                for m in read.get(k, []):
+                    add(m, False)
+        for k in wr:
+            add(wrote.get(k), True)
+            for m in read.get(k, []):
+                add(m, True)
+        for s in sorted(marks, key=lambda z: z == q):
+            need(q, (s, marks[s]))
+        count[sem] = count.get(sem, 0) + inc
+        fn().then_inc(T.sem[sem], inc)
+        mark = (sem, count[sem])
+        snap[mark] = dict(known[q])
+        for k in rd:
+            read.setdefault(k, []).append(mark)
+        for k in wr:
+            wrote[k] = mark
+            read[k] = []
+        return mark
+
+    V, S, P = g.vector, g.scalar, g.tensor
+
+    def ts(out, in0, s1, s2, o0, o1, rd, wr):
+        if o1 is None:
+            return op("v", lambda: V.tensor_scalar(out, in0, s1, None, o0), rd, wr)
+        return op("v", lambda: V.tensor_scalar(out, in0, s1, s2, o0, o1), rd, wr)
+
+    def tt(out, in0, in1, o, rd, wr):
+        return op("v", lambda: V.tensor_tensor(out, in0, in1, o), rd, wr)
+
+    def cp(out, in_, rd, wr):
+        return op("v", lambda: V.tensor_copy(out, in_), rd, wr)
+
+    def ms(ap, val, wr):
+        return op("v", lambda: V.memset(ap, val), [], wr)
+
+    def scan(out, d0, d1, init, o0, o1, rd, wr):
+        return op("v", lambda: V.tensor_tensor_scan(out, d0, d1, init, o0, o1), rd, wr)
+
+    def qz(codes, scales, in_, rd, wr):
+        return op("v", lambda: V.quantize_mx(codes, scales, in_), rd, wr)
+
+    def act(out, in_, fn, rd, wr, bias=None, scale=None):
+        if bias is None and scale is None:
+            return op("a", lambda: S.activation(out, in_, fn), rd, wr)
+        if bias is None:
+            return op("a", lambda: S.activation(out, in_, fn, scale=scale), rd, wr)
+        return op("a", lambda: S.activation(out, in_, fn, bias=bias, scale=scale), rd, wr)
+
+    def bank(b, n):
+        return T.ps[:, 512 * b:512 * b + n]
+
+    def mm(b, n, lq, lz, rq, rz, rd):
+        return op("p", lambda: P.matmul_mx(bank(b, n), lq, lz, rq, rz, True, True), rd, ["#%d" % b])
+
+    def iota(out, pat, base, cm, wr):
+        return op("g", lambda: g.iota(out, pat, base, cm, allow_small_or_imprecise_dtypes=True), [], wr)
+
+    def asel(out, in_, pat, cmp, fill, base, cm, rd, wr):
+        return op("g", lambda: g.affine_select(out, in_, pat, cmp, fill, base, cm), rd, wr)
+
+    def dma(q, sem, out, in_, rd, wr):
+        return op(q, lambda: Q[q].dma_start(out, in_), rd, wr, sem=sem, inc=16)
+
+    names = ["pc", "sm_", "r", "pw", "pw4", "sc", "nbias", "sg0", "sg", "h1", "h0", "f0", "h1b", "h0b", "k1", "k0",
+             "dka", "dkb", "dk4", "boost", "c8", "offk", "m21"]
+    col = {n: i for i, n in enumerate(names)}
+
+    def c(n):
+        return T.cs[:, col[n]:col[n] + 1]
+
+    def cs(n, in0, s1, s2, o0, o1, rd):
+        return ts(c(n), in0, s1, s2, o0, o1, rd, [n])
+
+    def ca(n, in_, scale, bias, rd):
+        return act(c(n), in_, AF.Identity, rd, [n], bias=bias, scale=scale)
+
+    def cols(buf, h, n=H):
+        return buf[:, H * h:H * h + n]
+
+    def const(i):
+        return T.cq[:, 128 * i:128 * i + 128], T.cz[:, 128 * i:128 * i + 128]
+
+    def unit(b):
+        return T.eq[:, 128 * b:128 * b + 128], T.ez[:, 128 * b:128 * b + 128]
+
+    def quant_x(h, first):
+        src = T.x0 if first else T.xs
+        rd = ["x0_%d" % h] if first else ["xs%d_%d" % (h, k) for k in range(4)]
+        qz(cols(T.xq, h), cols(T.xz, h), src[:, 4 * H * h:4 * H * h + 4 * H], rd, ["xq%d" % h])
+
+    def score(h):
+        mm(4 + h, H, T.uq[:], T.uz[:], cols(T.xq, h), cols(T.xz, h), ["uq", "xq%d" % h])
+
+    def unpack(b):
+        mm(b, C, unit(b)[0], unit(b)[1], T.xq[:], T.xz[:], ["eq%d" % b, "xq0", "xq1"])
+
+    def fcopy(b):
+        act(T.ff[:, C * b:C * b + C], bank(b, C), AF.Copy, ["#%d" % b], ["ff%d" % b])
+
+    def signs(h):
+        ts(T.bt[:, 4 * H * h:4 * H * h + 4 * H:4], bank(4 + h, H), 0.0, None, A.is_gt, None,
+           ["#%d" % (4 + h)] + ["btz%d" % i for i in range(4)], ["bt%d" % h])
+
+    def quant_signs(h):
+        n = H if h == 0 else H + 32
+        qz(cols(T.bq, h, n), cols(T.bz, h, n), T.bt[:, 4 * H * h:4 * H * h + 4 * n], ["bt%d" % h], ["bq%d" % h])
+
+    def diag_k(h):
+        scan(cols(T.dk, h), T.d0[:, 0:H], bank(4 + h, H), 0.0, A.add, A.max, ["d0", "#%d" % (4 + h)], ["dk%d" % h])
+
+    def ranks(bu, bo):
+        qz(T.iq[:], T.iz[:], T.it[:], ["it"], ["iq"])
+        mm(bo, 128, const(1)[0], const(1)[1], T.iq[:], T.iz[:], ["cq", "iq"])
+        mm(bu, 128, const(0)[0], const(0)[1], T.iq[:], T.iz[:], ["cq", "iq"])
+        for s in range(4):
+            scan(T.inc[:, s:120:5], T.ps[:, 512 * bo + s:512 * bo + 120:5], T.big[:], s - 4.0, A.add, A.min,
+                 ["#%d" % bo, "big"], ["inc%d" % s])
+        tt(T.bb[:, 0:120], T.inc[:, 0:120], bank(bu, 120), A.subtract, ["inc%d" % s for s in range(5)] + ["#%d" % bu], ["bb"])
+        scan(T.sm[:, 0:120], T.d1r[:], T.bb[:, 0:120], 0.0, A.add, A.max, ["d1r", "bb"], ["sm"])
+
+    def zero_signs(i):
+        act(T.bt[:, CP * i:CP * i + CP], T.et[:, 0:CP], AF.Identity, ["et"], ["btz%d" % i], bias=0.0, scale=0.0)
+
+    def quant_unit(b):
+        qz(unit(b)[0], unit(b)[1], T.et[:, 3 - b:515 - b], ["et"], ["eq%d" % b])
+
+    dma("sy", "lx0", T.x0[:, 0:4 * H], T.x[:, 0:4 * H], [], ["x0_0"])
+    dma("a", "lu", T.ub[:], T.u[:], [], ["ub"])
+    dma("sy", "lx1", T.x0[:, 4 * H:4 * C], T.x[:, 4 * H:4 * C], [], ["x0_1"])
+    dma("sy", "lwc", T.wq[:].bitcast(dt.uint8), T.wc[:], ["x0_1"], ["wq"])
+    dma("sy", "lws", T.wz[:], T.ws[:], [], ["wz"])
+    dma("sy", "lv", T.vb[:], T.v[:], [], ["vb"])
+
+    iota(T.p2[:], [[0, 1]], 1, 2, ["p2"])
+    ms(T.hf[:], 0.5, ["hf"])
+    ms(T.z8[:], 0.0, ["z8"])
+    iota(T.k16[:], [[1, 16]], 0, 0, ["k16"])
+    scan(T.v8[:], T.hf[:], T.z8[:], T.p2[:], A.mult, A.add, ["hf", "z8", "p2"], ["v8"])
+    ms(T.et[:], 0.0, ["et"])
+    ts(T.fi[:], T.v8[:], -0.5, None, A.add, None, ["v8"], ["fi"])
+    iota(T.q2[:], [[128, 4], [2, 32]], 1, 0, ["q2"])
+    asel(T.et[:, 3:515:4], T.et[:, 3:515:4], [[-1, 128]], A.not_equal, 1.0, 0, 1, ["et"], ["et"])
+    iota(T.ig[:], [[1, 8], [0, 16]], 0, 0, ["ig"])
+    ms(T.ct[:, 0:512], 0.0, ["ct0"])
+    cp(T.fl[:], T.fi[:], ["fi"], ["fl"])
+    pf, gf, af = T.fl[:, 0:1], T.fl[:, 4:5], T.fl[:, 5:6]
+    ts(T.t8[:], T.k16[:, 0:8], gf, 1.0, A.is_lt, A.add, ["k16", "fl"], ["t8"])
+    cs("r", gf, -16.0, pf, A.mult, A.add, ["fl"])
+    op("v", lambda: V.tensor_reduce(c("pw"), T.t8[:], AxisListType.X, A.mult), ["t8"], ["pw"])
+    ts(T.m3c[:, 0:3], T.k16[:, 0:3], c("r"), None, A.is_equal, None, ["k16", "r"], ["m3c"])
+    cs("pw4", c("pw"), 4.0, None, A.mult, None, ["pw"])
+    ca("nbias", c("pw"), -4.0 * MAGIC, 0.0, ["pw"])
+    cs("sg0", pf, 96.0, -2.0, A.is_ge, A.mult, ["fl"])
+    op("v", lambda: V.reciprocal(c("sc"), c("pw4")), ["pw4"], ["sc"])
+    m0, m1, m2 = T.m3c[:, 0:1], T.m3c[:, 1:2], T.m3c[:, 2:3]
+    ca("h1", m0, 1024.0, 0.0, ["m3c"])
+    ca("h0", m0, -512.0, 0.0, ["m3c"])
+    act(T.nm[:], T.q2[:], AF.Identity, ["q2", "sc"], ["nm"], bias=MAGIC, scale=c("sc"))
+    ca("boost", c("r"), -STEP, 15.0 * STEP, ["r"])
+    act(T.n2[:], T.nm[:], AF.Identity, ["nm", "pw4", "nbias"], ["n2"], bias=c("nbias"), scale=c("pw4"))
+    ms(T.ct[:, 512:1536], 0.0, ["ct1"])
+    cs("sg", c("sg0"), 1.0, c("pw"), A.add, A.mult, ["sg0", "pw"])
+    cs("f0", gf, 5.0, -2.0, A.is_equal, A.mult, ["fl"])
+    cs("k1", m0, 2.0, c("pw"), A.mult, A.mult, ["m3c", "pw"])
+    cs("dka", c("sg"), -0.25, 64.0, A.mult, A.add, ["sg"])
+    cs("h1b", c("f0"), 1.0, c("h1"), A.add, A.mult, ["f0", "h1"])
+    cs("m21", m1, 2.0, m2, A.mult, A.add, ["m3c"])
+    cs("dkb", c("dka"), m0, None, A.mult, None, ["dka", "m3c"])
+    tt(T.nb[:], T.q2[:], T.n2[:], A.is_gt, ["q2", "n2"], ["nb"])
+    ca("h0b", c("h1b"), -0.5, 0.0, ["h1b"])
+    ca("k0", c("k1"), -0.5, 0.0, ["k1"])
+    ts(T.g4[:], T.ig[:], gf, 4.0, A.is_equal, A.mult, ["ig", "fl"], ["g4"])
+    cs("dk4", c("m21"), 1.0 / 32, c("dkb"), A.mult, A.add, ["m21", "dkb"])
+    ts(T.d0a[:], T.k16[:], c("r"), -BIG, A.is_equal, A.mult, ["k16", "r"], ["d0a"])
+    op("v", lambda: V.tensor_reduce(c("sm_"), T.fl[:, 1:8], AxisListType.X, A.add), ["fl"], ["sm_"])
+    act(T.ko[:], T.nb[:, 0:128:32], AF.Identity, ["nb", "k1", "k0"], ["ko"], bias=c("k0"), scale=c("k1"))
+    act(T.ct[:, 0:512:4], T.nb[:], AF.Identity, ["nb", "h1", "h0", "ct0"], ["ctH0"], bias=c("h0"), scale=c("h1"))
+    act(T.ct[:, 512:1024:4], T.nb[:], AF.Identity, ["nb", "h1b", "h0b", "ct1"], ["ctH1"], bias=c("h0b"), scale=c("h1b"))
+    for a in range(4):
+        act(T.ct[:, 1024 + 128 * a:1152 + 128 * a:4], T.g4[:, 32 * a:32 * a + 32], AF.Identity, ["g4", "dk4", "ko", "ct1"],
+            ["ctK%d" % a], bias=T.ko[:, a:a + 1], scale=c("dk4"))
+    asel(T.ua[:], T.g4[:], [[-1, 128]], A.is_ge, 0.0, 0, 1, ["g4"], ["ua"])
+    asel(T.ct[:, 1:512:4], T.ua[:], [[-1, 128]], A.not_equal, -2048.0, 0, 1, ["ua", "ct0"], ["ctU"])
+    cp(T.ct[:, 513:1024:4], T.g4[:], ["g4", "ct1"], ["ctO"])
+    ts(T.d0b[:], T.d0a[:], STEP, None, A.add, None, ["d0a"], ["d0b"])
+    cs("pc", c("sm_"), -1.0, pf, A.mult, A.add, ["sm_", "fl"])
+    ts(T.lr[:], T.q2[:, 0:24], 0.0, c("r"), A.mult, A.add, ["q2", "r"], ["lr"])
+    ts(T.d2b[:], T.k16[:], c("r"), 2.0, A.not_equal, A.mult, ["k16", "r"], ["d2b"])
+    ms(T.bt[:, 0:2 * CP], 0.0, ["btz0", "btz1"])
+    zero_signs(2)
+    zero_signs(3)
+    act(T.d0[:], T.d0b[:, 0:16].indirect(T.lr[:]), AF.Copy, ["d0b", "lr"], ["d0"])
+    for i in (1, 0):
+        act(T.d1[:, CP * i:CP * i + C], T.et[:, 0:C], AF.Identity, ["et"], ["d1a%d" % i], bias=-1.0, scale=0.0)
+        iota(T.d1[:, CP * i + C + 1:CP * i + CP], [[0, 31]], 0, 0, ["d1b%d" % i])
+    iota(T.ji[:], [[1, C]], 0, 0, ["ji"])
+    iota(T.idp[:], [[16, 24]], DUMP, 0, ["idp"])
+    iota(T.thr[:], [[0, 128]], 1000000, 0, ["thr0", "thr1", "thr2", "thr3"])
+    iota(T.tab[:, 256:512], [[0, 256]], 0, 0, ["tabz"])
+    iota(T.ik[:], [[16, 8]], -2, 0, ["ik"])
+    iota(T.it[:], [[0, 512]], 0, 0, ["it"])
+    iota(T.big[:], [[0, 24]], 1000000, 0, ["big"])
+    iota(T.ios[:], [[0, 120]], 0, 0, ["ios"])
+    asel(T.d1r[:], T.ios[:], [[0, 24], [1, 5]], A.not_equal, -BIG, 0, 0, ["ios"], ["d1r"])
+    iota(T.win[:, SLOT0:SLOT0 + NS], [[0, NS]], 0, 0, ["win"])
+
+    quant_x(0, True)
+    qz(T.uq[:], T.uz[:], T.ub[:], ["ub"], ["uq"])
+    score(0)
+    quant_unit(0)
+    quant_x(1, True)
+    score(1)
+    quant_unit(1)
+    qz(T.cq[:], T.cz[:], T.ct[:], ["ctH0", "ctH1", "ctK0", "ctK1", "ctK2", "ctK3", "ctU", "ctO"], ["cq"])
+    signs(0)
+    ts(T.ini[:], T.k16[:, 0:2], c("pc"), 512.0, A.subtract, A.mult, ["k16", "pc"], ["ini"])
+    ts(T.d1[:, C:2 * CP:CP], T.k16[:, 0:2], c("pc"), 512.0, A.add, A.mult, ["k16", "pc"], ["d1c"])
+    ca("c8", af, 64.0, c("sg"), ["fl", "sg"])
+    act(T.inc[:, 4:120:5], T.idp[:], AF.Identity, ["idp", "r"], ["inc4"], bias=c("r"), scale=1.0)
+    ca("offk", c("c8"), -1.0, c("boost"), ["c8", "boost"])
+    act(T.jc[:], T.ji[:], AF.Identity, ["ji"], ["jc"], bias=float(C), scale=1.0 / 1024)
+    act(T.tg[:], T.k16[:, 0:4], AF.Identity, ["k16", "offk"], ["tg"], bias=c("offk"), scale=0.125)
+    act(T.d2[:], T.d2b[:, 0:16].indirect(T.lr[:]), AF.Copy, ["d2b", "lr"], ["d2"])
+
+    for t in range(R):
+        quant_signs(0)
+        mm(4, H, const(2)[0], const(2)[1], cols(T.bq, 0), cols(T.bz, 0), ["cq", "bq0"])
+        unpack(0)
+        signs(1)
+        quant_signs(1)
+        mm(5, H, const(2)[0], const(2)[1], cols(T.bq, 1), cols(T.bz, 1), ["cq", "bq1"])
+        mm(7, CP, const(1)[0], const(1)[1], T.bq[:], T.bz[:], ["cq", "bq0", "bq1"])
+        mm(6, CP, const(0)[0], const(0)[1], T.bq[:], T.bz[:], ["cq", "bq0", "bq1"])
+        unpack(1)
+        if t > 0:
+            fcopy(0)
+            fcopy(1)
+        diag_k(0)
+        diag_k(1)
+        if t == 0:
+            quant_unit(2)
+            quant_unit(3)
+        unpack(2)
+        unpack(3)
+        scan(T.hb[:, 32:448], bank(7, CP), T.d1[:, CP:2 * CP], T.ini[:, 0:1], A.min, A.add,
+             ["#7", "d1a1", "d1b1", "d1c", "ini"], ["hb", "hb1"])
+        ts(T.key[:], T.dk[:, 15:C:16], c("offk"), None, A.subtract, None, ["dk0", "dk1", "offk"], ["key"])
+        scan(T.hb[:, 0:416], bank(6, CP), T.d1[:, 0:CP], T.ini[:, 1:2], A.min, A.add,
+             ["#6", "d1a0", "d1b0", "d1c", "ini"], ["hb"])
+        ts(T.keyf[:], T.key[:], -1.0, None, A.mult, None, ["key"], ["keyf"])
+        op("v", lambda: V.transpose(T.tab[:, 0:64], T.hb[:, 384:448]), ["hb", "hb1"], ["tab0"])
+        tt(T.fr[:], T.dk[:, 15:C:16], T.keyf[:], A.add, ["dk0", "dk1", "keyf"], ["fr"])
+        act(T.tab[64:96, 64:128], T.tab[96:128, 0:64], AF.Copy, ["tab0"], ["tab1c"])
+        act(T.tab[96:128, 64:128], T.tab[64:96, 0:64], AF.Copy, ["tab0"], ["tab1d"])
+        cp(T.tab[0:32, 64:128], T.tab[32:64, 0:64], ["tab0"], ["tab1a"])
+        cp(T.tab[32:64, 64:128], T.tab[0:32, 0:64], ["tab0"], ["tab1b"])
+
+        def classes(s):
+            ts(T.thr[:, s:120:5], T.fr[:], T.tg[:, s:s + 1], BIG, A.not_equal, A.mult, ["fr", "tg"], ["thr%d" % s])
+        classes(0)
+        classes(1)
+        act(T.tab[64:128, 128:256], T.tab[0:64, 0:128], AF.Copy, ["tab0", "tab1a", "tab1b"], ["tab2b"])
+        cp(T.tab[0:64, 128:256], T.tab[64:128, 0:128], ["tab0", "tab1c", "tab1d"], ["tab2a"])
+        classes(2)
+        tab = ["tab0", "tab1a", "tab1b", "tab1c", "tab1d", "tab2a", "tab2b", "tabz", "key"]
+        act(T.sn[:], T.tab[:, 0:512].indirect(T.key[:]), AF.Sign, tab, ["sn"], bias=-0.5, scale=-1.0)
+        for b in range(0 if t == 0 else 2, 4):
+            fcopy(b)
+        for b in range(4):
+            act(T.nf[:, C * b:C * b + C], T.ff[:, C * b:C * b + C], AF.Copy, ["ff%d" % b], ["nf%d" % b], scale=-1.0)
+        if t == 0:
+            ts(T.ci[:], T.ik[:], c("r"), 0.2, A.add, A.mult, ["ik", "r"], ["ci"])
+        tt(T.mp[:], T.tab[:, 0:512].indirect(T.key[:]), T.jc[:], A.add, tab + ["jc"], ["mp"])
+        if t == 0:
+            ts(T.l2[:], T.ci[:], 23.0, 16.0, A.min, A.mult, ["ci"], ["l2"])
+        scan(T.dm[:, 1:C + 1], T.d2[:], T.sn[:], 0.0, A.mult, A.add, ["d2", "sn"], ["dm"])
+        classes(3)
+        thr = ["thr%d" % s for s in range(4)]
+        tt(T.it[:, 1:512:4], T.dm[:, 16:C + 16].indirect(T.l2[:]), T.thr[:], A.is_gt, ["dm", "l2"] + thr, ["it"])
+        ranks(6, 7)
+        ts(T.pos[:], T.sm[:, 4:120:5], -float(DUMP), None, A.add, None, ["sm"], ["pos"])
+        cp(T.win[:, 0:1984].indirect(T.pos[:]), T.mp[:], ["pos", "mp", "win"], ["win"])
+        scan(T.de[:], T.d0[:, 0:NS], T.win[:, SLOT0:SLOT0 + NS], 0.0, A.add, A.max, ["d0", "win"], ["de"])
+        ts(T.b16[:], T.de[:, 15:NS:16], c("boost"), None, A.subtract, None, ["de", "boost"], ["b16"])
+        ts(T.pi[:], T.de[:, 15:NS:16], 1024.0, None, A.mult, None, ["de"], ["pi"])
+        for b in range(4):
+            act(T.aa[:, NS * b:NS * b + NS], T.ff[:, C * b:C * b + C].indirect(T.b16[:]), AF.Copy,
+                ["ff%d" % b, "b16"], ["aa%d" % b])
+        ts(T.pb[:], T.pi[:], 1023, None, A.bitwise_and, None, ["pi"], ["pb"])
+        cp(T.a16[:], T.pb[:], ["pb"], ["a16"])
+        for b in range(4):
+            tt(T.ee[:, b:4 * NS:4], T.nf[:, C * b:C * b + C].indirect(T.a16[:]), T.aa[:, NS * b:NS * b + NS],
+               A.add, ["nf%d" % b, "a16", "aa%d" % b], ["ee%d" % b])
+        oq, oz, lq, lz = T["oq%d" % t], T["oz%d" % t], T["lq%d" % t], T["lz%d" % t]
+        sent = qz(oq[:], oz[:], T.ee[:], ["ee%d" % b for b in range(4)], ["oq%d" % t])
+        dst = T.cores[(rank + 1 + t) % N]
+        rid, pid = topo.addr(dst)[0], topo.addr(dst)[1]
+        mask = topo.mask(core, dst)
+        need("g", sent)
+        g.remote_dma(lq[:].bitcast(dt.uint8), oq[:].bitcast(dt.uint8), T.sem["arr%d" % t], T.sem.snt, pid, rid, mask)
+        g.remote_dma(lz[:], oz[:], T.sem["arr%d" % t], T.sem.snt, pid, rid, mask)
+        count["snt"] = count.get("snt", 0) + 2 * len(topo.engines(core, dst))
+        src = T.cores[(rank - 1 - t) % N]
+        wrote["l%d" % t] = ("arr%d" % t, 2 * len(topo.engines(src, core)))
+        ts(T.it[:, 1:512:4], T.thr[:], 0.0, None, A.is_equal, None, thr, ["it"])
+        ranks(4, 5)
+        ts(T.tq[:], T.sm[:, 4:120:5], -2127.5, 1.0 / NS, A.add, A.mult, ["sm"], ["tq"])
+        ts(T.tr[:], T.tq[:], -float(NS), -2048.0, A.mult, A.add, ["tq"], ["tr"])
+        tt(T.tv[:], T.tr[:], T.sm[:, 4:120:5], A.add, ["tr", "sm"], ["tv"])
+        cp(T.tk[:], T.tv[:], ["tv"], ["tk"])
+        if t + 1 < R:
+            ms(T.win[:, SLOT0:SLOT0 + NS], 0.0, ["win"])
+        if t == 0:
+            qz(T.vq[:], T.vz[:], T.vb[:], ["vb"], ["vq"])
+        for b in (0, 2, 1, 3):
+            mm(4 + b, NS, unit(b)[0], unit(b)[1], lq[:], lz[:], ["eq%d" % b, "l%d" % t])
+        for b in (0, 1):
+            cp(T.gg[:, NS * b:NS * b + NS], bank(4 + b, NS), ["#%d" % (4 + b)], ["gg%d" % b])
+        for b in (2, 3):
+            act(T.gg[:, NS * b:NS * b + NS], bank(4 + b, NS), AF.Copy, ["#%d" % (4 + b)], ["gg%d" % b])
+        by_scalar = ((2, 3), (2, 3, 1))
+        for h in range(2):
+            for b in by_scalar[h]:
+                act(T.ga[:, C * b + H * h:C * b + H * h + H],
+                    T.gg[:, NS * b:NS * b + NS].indirect(T.tk[:, 12 * h:12 * h + 12]), AF.Copy,
+                    ["gg%d" % b, "tk"], ["ga%d_%d" % (h, b)])
+        last = t + 1 == R
+
+        def zadd(h, b):
+            out = T.zt[:, 4 * H * h + b:4 * H * h + 4 * H:4]
+            if b in by_scalar[h]:
+                tt(out, T.ps[:, 512 * b + H * h:512 * b + H * h + H], T.ga[:, C * b + H * h:C * b + H * h + H], A.add,
+                   ["#%d" % b, "ga%d_%d" % (h, b)], ["zt%d_%d" % (h, b)])
+            else:
+                tt(out, T.gg[:, NS * b:NS * b + NS].indirect(T.tk[:, 12 * h:12 * h + 12]),
+                   T.ff[:, C * b + H * h:C * b + H * h + H], A.add,
+                   ["gg%d" % b, "tk", "ff%d" % b], ["zt%d_%d" % (h, b)])
+
+        def layer(h):
+            qz(cols(T.zq, h), cols(T.zz, h), T.zt[:, 4 * H * h:4 * H * h + 4 * H],
+               ["zt%d_%d" % (h, b) for b in range(4)], ["zq%d" % h])
+            for k in range(4):
+                bk = 4 * (1 - h) + k
+                mm(bk, H, T.wq[:, 128 * k:128 * k + 128], T.wz[:, 128 * k:128 * k + 128],
+                   cols(T.zq, h), cols(T.zz, h), ["wq", "wz", "zq%d" % h])
+                act(T.rr[:, C * k + H * h:C * k + H * h + H], bank(bk, H), AF.Relu, ["#%d" % bk], ["rr%d_%d" % (h, k)],
+                    scale=0.015625)
+
+        def xadd(h, k):
+            tt(T.xs[:, 4 * H * h + k:4 * H * h + 4 * H:4], T.rr[:, C * k + H * h:C * k + H * h + H],
+               T.zt[:, 4 * H * h + k:4 * H * h + 4 * H:4], A.add,
+               ["rr%d_%d" % (h, k), "zt%d_%d" % (h, k)], ["xs%d_%d" % (h, k)])
+
+        def state(h):
+            quant_x(h, False)
+            if not last:
+                score(h)
+            else:
+                mm(4 + h, H, T.vq[:], T.vz[:], cols(T.xq, h), cols(T.xz, h), ["vq", "xq%d" % h])
+                dma("sy", "st_sy", T.oc[:, 4 * H * h:4 * H * h + 4 * H], cols(T.xq, h).bitcast(dt.uint8), ["xq%d" % h], [])
+        for b in range(4):
+            zadd(0, b)
+        zadd(1, 0)
+        layer(0)
+        for b in (2, 3, 1):
+            zadd(1, b)
+        xadd(0, 0)
+        layer(1)
+        for k in (1, 2, 3):
+            xadd(0, k)
+        xadd(1, 0)
+        state(0)
+        for k in (1, 2, 3):
+            xadd(1, k)
+        if not last:
+            signs(0)
+        state(1)
+
+    act(cols(T.yy, 0), bank(4, H), AF.Copy, ["#4"], ["yy0"])
+    dma("a", "st_sc", T.y[:, 0:H], cols(T.yy, 0), ["yy0"], [])
+    cp(cols(T.yy, 1), bank(5, H), ["#5"], ["yy1"])
+    for k in range(4):
+        q, sem = (("a", "st_sc"), ("sy", "st_sy"))[k % 2]
+        dma(q, sem, T.osc[4 * k:4 * k + 4, :], T.xz[32 * k:32 * k + 4, :], ["xq0", "xq1"], [])
+    dma("a", "st_sc", T.y[:, H:C], cols(T.yy, 1), ["yy1"], [])
+    for s in ("v", "a", "p", "g", "snt", "st_sc", "st_sy"):
+        need("sy", (s, count[s]))

@@ -1,13 +1,17 @@
 from concourse.mybir import dt, AluOpType as A, AxisListType, ActivationFunctionType as AF
 
 N, C, R, NS = 4, 384, 3, 160
-H = C // 2
+W = C // 2
 CP = C + 32
 STEP = 1024.0
 BIG = float(2 ** 30)
-MAGIC = 1.5 * 2 ** 23
+KW = 256.0
+TINY = 1e-37
 DUMP = 1600
 SLOT0 = 2048 - DUMP
+FUSED = (2, 1)
+ORDER = ("g0 g1 z0.0123 z1.0 l0 r0 z1.123 l1 r1 x0.01 x1.0 s0 n0 x1.1 s1 q0 n1 k0 q1 a0 b0 k1 a1 f0 f1 b1 f2")
+LAST = "g0 g1 z0.0123 z1.0 l0 r0 z1.123 l1 r1 x0.01 x1.0 s0 x1.1 s1"
 F32, BF, I32, U16, CO, SC = "float32", "bfloat16", "int32", "uint16", "float8_e4m3fn_x4", "uint8"
 
 
@@ -20,35 +24,33 @@ SCRATCH = {
     "x0": _s(4 * C, BF), "ub": _s(512, BF), "vb": _s(512, BF),
     "wq": _s(512, CO), "wz": _s(512, SC), "uq": _s(128, CO), "uz": _s(128, SC), "vq": _s(128, CO), "vz": _s(128, SC),
     "et": _s(528, BF), "eq": _s(512, CO), "ez": _s(512, SC),
-    "ct": _s(1536, BF), "cq": _s(384, CO), "cz": _s(384, SC),
-    "xs": _s(4 * C, BF), "xq": _s(C, CO), "xz": _s(C, SC),
+    "ct": _s(516, BF), "cu": _s(512, BF), "cq": _s(512, CO), "cz": _s(512, SC),
+    "xq": _s(C, CO), "xz": _s(C, SC),
     "zt": _s(4 * C, BF), "zq": _s(C, CO), "zz": _s(C, SC),
-    "bt": _s(4 * CP, BF), "bq": _s(CP, CO), "bz": _s(CP, SC),
-    "it": _s(512, BF), "iq": _s(128, CO), "iz": _s(128, SC),
-    "ff": _s(4 * C, BF), "nf": _s(4 * C, BF), "gg": _s(4 * NS, BF), "ga": _s(4 * C, BF), "aa": _s(4 * NS, BF),
-    "ee": _s(4 * NS, BF), "rr": _s(4 * C, F32), "yy": _s(C, F32),
-    "hb": _s(448, F32), "tab": _s(512, F32), "dk": _s(C, F32), "mp": _s(C, F32), "dm": _s(C + 16, BF), "sn": _s(C, BF),
-    "win": _s(1984, F32), "de": _s(NS, F32),
+    "bt": _s(4 * (W + 32), BF), "bq": _s(CP, CO), "bz": _s(CP, SC),
+    "it": _s(1024, BF), "iq": _s(256, CO), "iz": _s(256, SC),
+    "nf": _s(4 * C, BF), "gg": _s(4 * NS, BF), "ga": _s(4 * C, BF), "aa": _s(4 * NS, BF),
+    "ee": _s(1024, BF), "rr": _s(4 * C, F32), "yy": _s(C, F32),
+    "ha": _s(2 * W, F32), "hb": _s(W + 64, F32), "tab": _s(512, F32), "dk": _s(C, F32), "mp": _s(C, F32),
+    "dm": _s(C + 16, BF), "sn": _s(C, BF), "win": _s(1984, F32), "de": _s(NS, F32),
     "key": _s(24, U16), "keyf": _s(24, F32), "fr": _s(24, F32), "thr": _s(128, F32),
     "inc": _s(128, F32), "bb": _s(128, F32), "sm": _s(128, F32),
-    "pos": _s(24, U16), "a16": _s(10, U16), "pi": _s(10, I32), "pb": _s(10, I32), "b16": _s(10, U16),
+    "pos": _s(24, U16), "a16": _s(40, U16), "pi": _s(40, I32), "pb": _s(40, I32), "b16": _s(40, U16),
     "tq": _s(24, I32), "tr": _s(24, F32), "tv": _s(24, F32), "tk": _s(24, U16),
-    "cs": _s(64, F32), "p2": _s(1, F32), "k16": _s(16, F32), "hf": _s(8, F32), "z8": _s(8, F32), "v8": _s(8, F32),
-    "fi": _s(8, I32), "fl": _s(8, F32), "t8": _s(8, F32), "m3c": _s(4, F32), "ini": _s(2, F32), "ko": _s(4, F32),
-    "tg": _s(4, F32), "q2": _s(128, F32), "nm": _s(128, F32), "n2": _s(128, F32), "nb": _s(128, BF),
-    "d0a": _s(16, F32), "d0b": _s(16, F32), "lr": _s(24, U16), "d0": _s(C, BF), "d2b": _s(16, F32), "d2": _s(C, BF),
-    "ji": _s(C, F32), "jc": _s(C, F32), "d1": _s(2 * CP, BF),
-    "ig": _s(128, F32), "g4": _s(128, F32), "ua": _s(128, F32), "ios": _s(120, F32), "d1r": _s(120, F32),
+    "cs": _s(32, F32), "pv": _s(8, F32), "gi": _s(1, I32), "k4": _s(4, F32), "t8": _s(7, F32),
+    "ko": _s(4, F32), "tg": _s(4, F32), "q2": _s(128, F32), "n2": _s(128, F32), "nb": _s(128, BF),
+    "j16": _s(C, BF), "d0": _s(W, BF), "d2": _s(C, BF), "jc": _s(C, F32), "d1": _s(W + 32, BF),
+    "ig": _s(128, F32), "d4": _s(NS, BF), "qi": _s(1, I32), "d1r": _s(120, F32),
     "big": _s(24, F32), "idp": _s(24, F32), "ik": _s(8, F32), "ci": _s(8, I32), "l2": _s(8, U16),
 }
 for _t in range(R):
-    SCRATCH["oq%d" % _t] = _s(NS, CO)
-    SCRATCH["oz%d" % _t] = _s(NS, SC)
+    SCRATCH["oq%d" % _t] = _s(256, CO)
+    SCRATCH["oz%d" % _t] = _s(256, SC)
     SCRATCH["lq%d" % _t] = _s(NS, CO)
     SCRATCH["lz%d" % _t] = _s(NS, SC)
 
 SEMAPHORES = ["v", "a", "p", "g", "lx0", "lx1", "lu", "lv", "lwc", "lws", "arr0", "arr1", "arr2", "snt",
-              "st_sy", "st_sc"]
+              "st_sy", "st_sc", "gd"]
 
 
 def rank_program(g, core, T, topo):
@@ -132,8 +134,8 @@ def rank_program(g, core, T, topo):
             return op("a", lambda: S.activation(out, in_, fn, scale=scale), rd, wr)
         return op("a", lambda: S.activation(out, in_, fn, bias=bias, scale=scale), rd, wr)
 
-    def bank(b, n):
-        return T.ps[:, 512 * b:512 * b + n]
+    def bank(b, n, a=0):
+        return T.ps[:, 512 * b + a:512 * b + a + n]
 
     def mm(b, n, lq, lz, rq, rz, rd):
         return op("p", lambda: P.matmul_mx(bank(b, n), lq, lz, rq, rz, True, True), rd, ["#%d" % b])
@@ -147,8 +149,8 @@ def rank_program(g, core, T, topo):
     def dma(q, sem, out, in_, rd, wr):
         return op(q, lambda: Q[q].dma_start(out, in_), rd, wr, sem=sem, inc=16)
 
-    names = ["pc", "sm_", "r", "pw", "pw4", "sc", "nbias", "sg0", "sg", "h1", "h0", "f0", "h1b", "h0b", "k1", "k0",
-             "dka", "dkb", "dk4", "boost", "c8", "offk", "m21"]
+    names = ["r", "pw", "mg", "sg0", "sg", "w0", "w1", "f0", "k1", "c3", "r4", "a3", "own", "boost", "c8", "offk", "ofs",
+             "q4", "el", "b4"]
     col = {n: i for i, n in enumerate(names)}
 
     def c(n):
@@ -160,314 +162,353 @@ def rank_program(g, core, T, topo):
     def ca(n, in_, scale, bias, rd):
         return act(c(n), in_, AF.Identity, rd, [n], bias=bias, scale=scale)
 
-    def cols(buf, h, n=H):
-        return buf[:, H * h:H * h + n]
-
     def const(i):
         return T.cq[:, 128 * i:128 * i + 128], T.cz[:, 128 * i:128 * i + 128]
 
     def unit(b):
         return T.eq[:, 128 * b:128 * b + 128], T.ez[:, 128 * b:128 * b + 128]
 
-    def quant_x(h, first):
-        src = T.x0 if first else T.xs
-        rd = ["x0_%d" % h] if first else ["xs%d_%d" % (h, k) for k in range(4)]
-        qz(cols(T.xq, h), cols(T.xz, h), src[:, 4 * H * h:4 * H * h + 4 * H], rd, ["xq%d" % h])
+    def cols(buf, p, n=W):
+        return buf[:, W * p:W * p + n]
 
-    def score(h):
-        mm(4 + h, H, T.uq[:], T.uz[:], cols(T.xq, h), cols(T.xz, h), ["uq", "xq%d" % h])
+    def tile(buf, p):
+        return buf[:, 4 * W * p:4 * W * p + 4 * W]
+
+    def plane(buf, p, k):
+        return buf[:, 4 * W * p + k:4 * W * p + 4 * W:4]
+
+    def planes(name, p):
+        return ["%s%d_%d" % (name, p, k) for k in range(4)]
+
+    score_bank, key_bank, word_bank = (4, 0), (5, 1), ((6, 7), (3, 2))
+
+    def score(p):
+        b = score_bank[p]
+        mm(b, W, T.uq[:], T.uz[:], cols(T.xq, p), cols(T.xz, p), ["uq", "xq%d" % p])
+
+    def sign(p):
+        b = score_bank[p]
+        act(T.bt[:, 0:4 * W:4], bank(b, W), AF.Sign, ["#%d" % b, "btz"], ["bt"], bias=-TINY, scale=1.0)
+
+    def signs(p, tail=0):
+        n = W + tail
+        qz(cols(T.bq, p, n), cols(T.bz, p, n), T.bt[:, 0:4 * n], ["bt"], ["bq%d" % p])
+        mm(key_bank[p], W, const(2)[0], const(2)[1], cols(T.bq, p), cols(T.bz, p), ["cq2", "bq%d" % p])
+        n = W + 32 * p
+        for i in (1, 0):
+            mm(word_bank[p][i], n, const(i)[0], const(i)[1], cols(T.bq, p, n), cols(T.bz, p, n), ["cq%d" % i, "bq%d" % p])
+
+    def diag_k(p):
+        b = key_bank[p]
+        scan(cols(T.dk, p), T.d0[:, 0:W], bank(b, W), 0.0, A.add, A.max, ["d0", "#%d" % b], ["dk%d" % p])
+
+    def words(p, i):
+        b = word_bank[p][i]
+        if p == 0:
+            scan(cols(T.ha, i), bank(b, W), T.d1[:, 0:W], 0.0, A.min, A.add, ["#%d" % b, "d1"], ["ha%d" % i])
+        else:
+            scan(T.hb[:, 32 * i:32 * i + W + 32], bank(b, W + 32), T.d1[:], T.ha[:, W * i + W - 1:W * i + W],
+                 A.min, A.add, ["#%d" % b, "d1", "ha%d" % i], ["hb"])
 
     def unpack(b):
         mm(b, C, unit(b)[0], unit(b)[1], T.xq[:], T.xz[:], ["eq%d" % b, "xq0", "xq1"])
 
     def fcopy(b):
-        act(T.ff[:, C * b:C * b + C], bank(b, C), AF.Copy, ["#%d" % b], ["ff%d" % b])
+        act(T.nf[:, b:4 * C:4], bank(b, C), AF.Copy, ["#%d" % b], ["nf%d" % b], scale=-1.0)
 
-    def signs(h):
-        ts(T.bt[:, 4 * H * h:4 * H * h + 4 * H:4], bank(4 + h, H), 0.0, None, A.is_gt, None,
-           ["#%d" % (4 + h)] + ["btz%d" % i for i in range(4)], ["bt%d" % h])
+    def flags(i):
+        return T.it[:, 512 * i + 3:512 * i + 512:4]
 
-    def quant_signs(h):
-        n = H if h == 0 else H + 32
-        qz(cols(T.bq, h, n), cols(T.bz, h, n), T.bt[:, 4 * H * h:4 * H * h + 4 * n], ["bt%d" % h], ["bq%d" % h])
+    def ranks(i, bu, bo):
+        iq, iz = T.iq[:, 128 * i:128 * i + 128], T.iz[:, 128 * i:128 * i + 128]
+        qz(iq, iz, T.it[:, 512 * i:512 * i + 512], ["it%d" % i], ["iq%d" % i])
+        mm(bo, 128, const(0)[0], const(0)[1], iq, iz, ["cq0", "iq%d" % i])
+        mm(bu, 128, const(3)[0], const(3)[1], iq, iz, ["cq3", "iq%d" % i])
 
-    def diag_k(h):
-        scan(cols(T.dk, h), T.d0[:, 0:H], bank(4 + h, H), 0.0, A.add, A.max, ["d0", "#%d" % (4 + h)], ["dk%d" % h])
-
-    def ranks(bu, bo):
-        qz(T.iq[:], T.iz[:], T.it[:], ["it"], ["iq"])
-        mm(bo, 128, const(1)[0], const(1)[1], T.iq[:], T.iz[:], ["cq", "iq"])
-        mm(bu, 128, const(0)[0], const(0)[1], T.iq[:], T.iz[:], ["cq", "iq"])
-        for s in range(4):
-            scan(T.inc[:, s:120:5], T.ps[:, 512 * bo + s:512 * bo + 120:5], T.big[:], s - 4.0, A.add, A.min,
+    def counts(bo, classes):
+        for s in classes:
+            scan(T.inc[:, s:120:5], T.ps[:, 512 * bo + s:512 * bo + 120:5], T.big[:], s / 4 - 1.0, A.add, A.min,
                  ["#%d" % bo, "big"], ["inc%d" % s])
+
+    def within(bu):
         tt(T.bb[:, 0:120], T.inc[:, 0:120], bank(bu, 120), A.subtract, ["inc%d" % s for s in range(5)] + ["#%d" % bu], ["bb"])
+
+    def choose():
         scan(T.sm[:, 0:120], T.d1r[:], T.bb[:, 0:120], 0.0, A.add, A.max, ["d1r", "bb"], ["sm"])
 
-    def zero_signs(i):
-        act(T.bt[:, CP * i:CP * i + CP], T.et[:, 0:CP], AF.Identity, ["et"], ["btz%d" % i], bias=0.0, scale=0.0)
+    def fill(out, n, val, wr):
+        act(out, T.et[:, 0:n], AF.Identity, ["et"], wr, bias=val, scale=0.0)
 
     def quant_unit(b):
         qz(unit(b)[0], unit(b)[1], T.et[:, 3 - b:515 - b], ["et"], ["eq%d" % b])
 
-    dma("sy", "lx0", T.x0[:, 0:4 * H], T.x[:, 0:4 * H], [], ["x0_0"])
     dma("a", "lu", T.ub[:], T.u[:], [], ["ub"])
-    dma("sy", "lx1", T.x0[:, 4 * H:4 * C], T.x[:, 4 * H:4 * C], [], ["x0_1"])
+    dma("sy", "lx0", tile(T.x0, 0), tile(T.x, 0), [], ["x0_0"])
+    dma("sy", "lx1", tile(T.x0, 1), tile(T.x, 1), [], ["x0_1"])
     dma("sy", "lwc", T.wq[:].bitcast(dt.uint8), T.wc[:], ["x0_1"], ["wq"])
     dma("sy", "lws", T.wz[:], T.ws[:], [], ["wz"])
     dma("sy", "lv", T.vb[:], T.v[:], [], ["vb"])
 
-    iota(T.p2[:], [[0, 1]], 1, 2, ["p2"])
-    ms(T.hf[:], 0.5, ["hf"])
-    ms(T.z8[:], 0.0, ["z8"])
-    iota(T.k16[:], [[1, 16]], 0, 0, ["k16"])
-    scan(T.v8[:], T.hf[:], T.z8[:], T.p2[:], A.mult, A.add, ["hf", "z8", "p2"], ["v8"])
-    ms(T.et[:], 0.0, ["et"])
-    ts(T.fi[:], T.v8[:], -0.5, None, A.add, None, ["v8"], ["fi"])
+    pf = T.pv[:, 0:1]
+    iota(T.pv[:], [[-16, 8]], 0, 1, ["pv"])
     iota(T.q2[:], [[128, 4], [2, 32]], 1, 0, ["q2"])
-    asel(T.et[:, 3:515:4], T.et[:, 3:515:4], [[-1, 128]], A.not_equal, 1.0, 0, 1, ["et"], ["et"])
-    iota(T.ig[:], [[1, 8], [0, 16]], 0, 0, ["ig"])
-    ms(T.ct[:, 0:512], 0.0, ["ct0"])
-    cp(T.fl[:], T.fi[:], ["fi"], ["fl"])
-    pf, gf, af = T.fl[:, 0:1], T.fl[:, 4:5], T.fl[:, 5:6]
-    ts(T.t8[:], T.k16[:, 0:8], gf, 1.0, A.is_lt, A.add, ["k16", "fl"], ["t8"])
-    cs("r", gf, -16.0, pf, A.mult, A.add, ["fl"])
+    iota(T.ig[:], [[16, 8], [0, 16]], 0, -1, ["ig"])
+    iota(T.j16[:], [[0, 24], [1, 16]], 0, 0, ["j16"])
+    ms(T.et[:], 0.0, ["et"])
+    fill(T.bt[:, 0:512], 512, 0.0, ["btz0"])
+    fill(T.bt[:, 512:896], 384, 0.0, ["btz"])
+    ts(T.t8[:], T.pv[:, 1:8], 0.0, 1.0, A.is_ge, A.add, ["pv"], ["t8"])
+    ts(T.gi[:], pf, -7.5, 1.0 / 16, A.add, A.mult, ["pv"], ["gi"])
     op("v", lambda: V.tensor_reduce(c("pw"), T.t8[:], AxisListType.X, A.mult), ["t8"], ["pw"])
-    ts(T.m3c[:, 0:3], T.k16[:, 0:3], c("r"), None, A.is_equal, None, ["k16", "r"], ["m3c"])
-    cs("pw4", c("pw"), 4.0, None, A.mult, None, ["pw"])
-    ca("nbias", c("pw"), -4.0 * MAGIC, 0.0, ["pw"])
-    cs("sg0", pf, 96.0, -2.0, A.is_ge, A.mult, ["fl"])
-    op("v", lambda: V.reciprocal(c("sc"), c("pw4")), ["pw4"], ["sc"])
-    m0, m1, m2 = T.m3c[:, 0:1], T.m3c[:, 1:2], T.m3c[:, 2:3]
-    ca("h1", m0, 1024.0, 0.0, ["m3c"])
-    ca("h0", m0, -512.0, 0.0, ["m3c"])
-    act(T.nm[:], T.q2[:], AF.Identity, ["q2", "sc"], ["nm"], bias=MAGIC, scale=c("sc"))
-    ca("boost", c("r"), -STEP, 15.0 * STEP, ["r"])
-    act(T.n2[:], T.nm[:], AF.Identity, ["nm", "pw4", "nbias"], ["n2"], bias=c("nbias"), scale=c("pw4"))
-    ms(T.ct[:, 512:1536], 0.0, ["ct1"])
-    cs("sg", c("sg0"), 1.0, c("pw"), A.add, A.mult, ["sg0", "pw"])
-    cs("f0", gf, 5.0, -2.0, A.is_equal, A.mult, ["fl"])
-    cs("k1", m0, 2.0, c("pw"), A.mult, A.mult, ["m3c", "pw"])
-    cs("dka", c("sg"), -0.25, 64.0, A.mult, A.add, ["sg"])
-    cs("h1b", c("f0"), 1.0, c("h1"), A.add, A.mult, ["f0", "h1"])
-    cs("m21", m1, 2.0, m2, A.mult, A.add, ["m3c"])
-    cs("dkb", c("dka"), m0, None, A.mult, None, ["dka", "m3c"])
-    tt(T.nb[:], T.q2[:], T.n2[:], A.is_gt, ["q2", "n2"], ["nb"])
-    ca("h0b", c("h1b"), -0.5, 0.0, ["h1b"])
-    ca("k0", c("k1"), -0.5, 0.0, ["k1"])
-    ts(T.g4[:], T.ig[:], gf, 4.0, A.is_equal, A.mult, ["ig", "fl"], ["g4"])
-    cs("dk4", c("m21"), 1.0 / 32, c("dkb"), A.mult, A.add, ["m21", "dkb"])
-    ts(T.d0a[:], T.k16[:], c("r"), -BIG, A.is_equal, A.mult, ["k16", "r"], ["d0a"])
-    op("v", lambda: V.tensor_reduce(c("sm_"), T.fl[:, 1:8], AxisListType.X, A.add), ["fl"], ["sm_"])
-    act(T.ko[:], T.nb[:, 0:128:32], AF.Identity, ["nb", "k1", "k0"], ["ko"], bias=c("k0"), scale=c("k1"))
-    act(T.ct[:, 0:512:4], T.nb[:], AF.Identity, ["nb", "h1", "h0", "ct0"], ["ctH0"], bias=c("h0"), scale=c("h1"))
-    act(T.ct[:, 512:1024:4], T.nb[:], AF.Identity, ["nb", "h1b", "h0b", "ct1"], ["ctH1"], bias=c("h0b"), scale=c("h1b"))
+    cs("r", T.gi[:], -16.0, pf, A.mult, A.add, ["gi", "pv"])
+    cs("mg", c("pw"), 6.0 * 2 ** 23, None, A.mult, None, ["pw"])
+    cs("sg0", c("pw"), 64.0, -1.0, A.is_ge, A.mult, ["pw"])
+    ts(T.n2[:], T.q2[:], c("mg"), c("mg"), A.add, A.subtract, ["q2", "mg"], ["n2"])
+    cs("sg", c("sg0"), 0.5, c("pw"), A.add, A.mult, ["sg0", "pw"])
+    tt(T.n2[:], T.q2[:], T.n2[:], A.subtract, ["q2", "n2"], ["n2"])
+    cs("w0", c("r"), 0.0, KW, A.is_equal, A.mult, ["r"])
+    act(T.nb[:], T.n2[:], AF.Sign, ["n2"], ["nb"])
+    cs("f0", c("pw"), 32.0, -2.0, A.is_equal, A.mult, ["pw"])
+    cs("k1", c("r"), 0.0, c("pw"), A.is_equal, A.mult, ["r", "pw"])
+    cs("w1", c("f0"), 1.0, c("w0"), A.add, A.mult, ["f0", "w0"])
+    ts(T.ct[:, 3:512:4], T.ig[:], c("r"), 0.0, A.add, A.is_equal, ["ig", "r"], ["ct3"])
+    act(c("c3"), c("r"), AF.Relu, ["r"], ["c3"], bias=3.0 / 16, scale=-1.0 / 16)
+    cs("a3", c("sg"), -1.0 / KW, (128.0 - 3.0 / 16) / KW, A.mult, A.add, ["sg"])
+    ts(T.ko[:], T.nb[:, 0:128:32], c("k1"), 0.5, A.mult, A.mult, ["nb", "k1"], ["ko"])
+    cs("own", c("a3"), c("w0"), c("c3"), A.mult, A.add, ["a3", "w0", "c3"])
+    for i in range(2):
+        act(T.ct[:, i:512:4], T.nb[:], AF.Identity, ["nb", "w%d" % i], ["ct%d" % i], bias=0.0, scale=c("w%d" % i))
+    ms(T.ct[:, 512:516], 0.0, ["ct4"])
     for a in range(4):
-        act(T.ct[:, 1024 + 128 * a:1152 + 128 * a:4], T.g4[:, 32 * a:32 * a + 32], AF.Identity, ["g4", "dk4", "ko", "ct1"],
-            ["ctK%d" % a], bias=T.ko[:, a:a + 1], scale=c("dk4"))
-    asel(T.ua[:], T.g4[:], [[-1, 128]], A.is_ge, 0.0, 0, 1, ["g4"], ["ua"])
-    asel(T.ct[:, 1:512:4], T.ua[:], [[-1, 128]], A.not_equal, -2048.0, 0, 1, ["ua", "ct0"], ["ctU"])
-    cp(T.ct[:, 513:1024:4], T.g4[:], ["g4", "ct1"], ["ctO"])
-    ts(T.d0b[:], T.d0a[:], STEP, None, A.add, None, ["d0a"], ["d0b"])
-    cs("pc", c("sm_"), -1.0, pf, A.mult, A.add, ["sm_", "fl"])
-    ts(T.lr[:], T.q2[:, 0:24], 0.0, c("r"), A.mult, A.add, ["q2", "r"], ["lr"])
-    ts(T.d2b[:], T.k16[:], c("r"), 2.0, A.not_equal, A.mult, ["k16", "r"], ["d2b"])
-    ms(T.bt[:, 0:2 * CP], 0.0, ["btz0", "btz1"])
-    zero_signs(2)
-    zero_signs(3)
-    act(T.d0[:], T.d0b[:, 0:16].indirect(T.lr[:]), AF.Copy, ["d0b", "lr"], ["d0"])
-    for i in (1, 0):
-        act(T.d1[:, CP * i:CP * i + C], T.et[:, 0:C], AF.Identity, ["et"], ["d1a%d" % i], bias=-1.0, scale=0.0)
-        iota(T.d1[:, CP * i + C + 1:CP * i + CP], [[0, 31]], 0, 0, ["d1b%d" % i])
-    iota(T.ji[:], [[1, C]], 0, 0, ["ji"])
-    iota(T.idp[:], [[16, 24]], DUMP, 0, ["idp"])
-    iota(T.thr[:], [[0, 128]], 1000000, 0, ["thr0", "thr1", "thr2", "thr3"])
-    iota(T.tab[:, 256:512], [[0, 256]], 0, 0, ["tabz"])
-    iota(T.ik[:], [[16, 8]], -2, 0, ["ik"])
-    iota(T.it[:], [[0, 512]], 0, 0, ["it"])
-    iota(T.big[:], [[0, 24]], 1000000, 0, ["big"])
-    iota(T.ios[:], [[0, 120]], 0, 0, ["ios"])
-    asel(T.d1r[:], T.ios[:], [[0, 24], [1, 5]], A.not_equal, -BIG, 0, 0, ["ios"], ["d1r"])
-    iota(T.win[:, SLOT0:SLOT0 + NS], [[0, NS]], 0, 0, ["win"])
-
-    quant_x(0, True)
+        ts(T.ct[:, 128 * a + 2:128 * a + 128:4], T.ct[:, 128 * a + 3:128 * a + 128:4], c("own"), T.ko[:, a:a + 1],
+           A.mult, A.add, ["ct3", "own", "ko"], ["ct2_%d" % a])
+    fill(T.d1[:, 0:W], W, -1.0, ["d1a"])
+    fill(T.d1[:, W + 1:W + 32], 31, 0.0, ["d1b"])
+    fill(T.d1[:, W:W + 1], 1, 8 * KW, ["d1"])
     qz(T.uq[:], T.uz[:], T.ub[:], ["ub"], ["uq"])
+    iota(T.k4[:], [[1, 4]], 0, 0, ["k4"])
+    iota(T.jc[:], [[1, C]], 0, 0, ["jc"])
+    iota(T.tab[:, 256:512], [[0, 256]], 0, 0, ["tabz"])
+    asel(T.et[:, 3:515:4], T.et[:, 3:515:4], [[-1, 128]], A.not_equal, 1.0, 0, 1, ["et"], ["et"])
+    iota(T.cu[:], [[0, 512]], 0, 0, ["cu"])
+
+    cts = ["ct0", "ct1", "ct3", "ct4"] + ["ct2_%d" % a for a in range(4)]
+    qz(cols(T.xq, 0), cols(T.xz, 0), tile(T.x0, 0), ["x0_0"], ["xq0"])
     score(0)
-    quant_unit(0)
-    quant_x(1, True)
+    sign(0)
+    ts(T.d2[:], T.j16[:], c("r"), 2.0, A.not_equal, A.mult, ["j16", "r"], ["d2"])
+    for i in (2, 1, 0):
+        qz(const(i)[0], const(i)[1], T.ct[:, i:i + 512], cts, ["cq%d" % i])
+    act(T.d0[:], T.d2[:, 0:W], AF.Identity, ["d2"], ["d0"], bias=-31 * STEP, scale=16 * STEP)
+    act(T.jc[:], T.jc[:], AF.Identity, ["jc"], ["jc"], bias=float(C), scale=1.0 / 4096)
+    qz(cols(T.xq, 1), cols(T.xz, 1), tile(T.x0, 1), ["x0_1"], ["xq1"])
     score(1)
-    quant_unit(1)
-    qz(T.cq[:], T.cz[:], T.ct[:], ["ctH0", "ctH1", "ctK0", "ctK1", "ctK2", "ctK3", "ctU", "ctO"], ["cq"])
     signs(0)
-    ts(T.ini[:], T.k16[:, 0:2], c("pc"), 512.0, A.subtract, A.mult, ["k16", "pc"], ["ini"])
-    ts(T.d1[:, C:2 * CP:CP], T.k16[:, 0:2], c("pc"), 512.0, A.add, A.mult, ["k16", "pc"], ["d1c"])
-    ca("c8", af, 64.0, c("sg"), ["fl", "sg"])
-    act(T.inc[:, 4:120:5], T.idp[:], AF.Identity, ["idp", "r"], ["inc4"], bias=c("r"), scale=1.0)
-    ca("offk", c("c8"), -1.0, c("boost"), ["c8", "boost"])
-    act(T.jc[:], T.ji[:], AF.Identity, ["ji"], ["jc"], bias=float(C), scale=1.0 / 1024)
-    act(T.tg[:], T.k16[:, 0:4], AF.Identity, ["k16", "offk"], ["tg"], bias=c("offk"), scale=0.125)
-    act(T.d2[:], T.d2b[:, 0:16].indirect(T.lr[:]), AF.Copy, ["d2b", "lr"], ["d2"])
+    sign(1)
+    ca("boost", c("r"), -STEP, 15.0 * STEP, ["r"])
+    ca("c8", c("sg"), -1.0, -255.6875, ["sg"])
+    ca("r4", c("r"), 0.25, 0.0, ["r"])
+    ca("offk", c("c8"), 1.0, c("boost"), ["c8", "boost"])
+    ca("ofs", c("offk"), -BIG, 0.0, ["offk"])
+    act(T.tg[:], T.k4[:], AF.Identity, ["k4", "ofs"], ["tg"], bias=c("ofs"), scale=-BIG / 8)
+    fill(T.it[:, 512:1024], 512, 0.0, ["it1"])
+    asel(T.cu[:, 3:512:4], T.ct[:, 3:512:4], [[-1, 128]], A.is_ge, 0.0, 0, 1, ["ct3", "cu"], ["cu"])
+    asel(T.cu[:, 3:512:4], T.cu[:, 3:512:4], [[-1, 128]], A.not_equal, -512.0, 0, 1, ["cu"], ["cu"])
+    iota(T.ik[:], [[16, 8]], -2, 0, ["ik"])
+    iota(T.thr[:, 4:128:5], [[0, 25]], 1000000, 0, ["thr4"])
+    iota(T.thr[:, 120:128], [[0, 8]], 1000000, 0, ["thr4"])
+    iota(T.it[:, 0:512], [[0, 512]], 0, 0, ["it0"])
+    iota(T.big[:], [[0, 24]], 1000000, 0, ["big"])
+    iota(T.idp[:], [[16, 24]], DUMP, 0, ["idp"])
+    iota(T.d1r[:], [[0, 120]], 0, 0, ["d1r"])
+    iota(T.d1r[:, 0:120:5], [[0, 24]], -1000000, 0, ["d1r"])
+    iota(T.win[:, SLOT0:SLOT0 + NS], [[0, NS]], 0, 0, ["win"])
+    iota(T.d4[:], [[0, NS // 4], [1, 4]], 0, 0, ["d4"])
+    for h in range(2):
+        iota(T.ee[:, 512 * h + 2 * NS:512 * h + 512], [[0, 512 - 2 * NS]], 0, 0, ["ez%d" % h])
+
+    def classes(s):
+        act(T.thr[:, s:120:5], T.fr[:], AF.Abs, ["fr", "tg"], ["thr%d" % s], bias=T.tg[:, s:s + 1], scale=BIG)
+
+    def split(i):
+        dks = ["dk0", "dk1"]
+        if i == 0:
+            ts(T.key[:], T.dk[:, 15:C:16], c("offk"), None, A.subtract, None, dks + ["offk"], ["key"])
+        elif i == 1:
+            ts(T.keyf[:], T.key[:], -1.0, None, A.mult, None, ["key"], ["keyf"])
+        else:
+            tt(T.fr[:], T.dk[:, 15:C:16], T.keyf[:], A.add, dks + ["keyf"], ["fr"])
+            classes(0)
+            classes(1)
+    listing = {"n": sign, "q": signs, "k": diag_k, "a": lambda p: words(p, 1), "b": lambda p: words(p, 0), "f": split}
+    quant_unit(0)
+    diag_k(0)
+    signs(1, 32)
+    for step in "a0 b0 k1 a1 f0 f1 b1 f2".split():
+        listing[step[0]](int(step[1]))
 
     for t in range(R):
-        quant_signs(0)
-        mm(4, H, const(2)[0], const(2)[1], cols(T.bq, 0), cols(T.bz, 0), ["cq", "bq0"])
-        unpack(0)
-        signs(1)
-        quant_signs(1)
-        mm(5, H, const(2)[0], const(2)[1], cols(T.bq, 1), cols(T.bz, 1), ["cq", "bq1"])
-        mm(7, CP, const(1)[0], const(1)[1], T.bq[:], T.bz[:], ["cq", "bq0", "bq1"])
-        mm(6, CP, const(0)[0], const(0)[1], T.bq[:], T.bz[:], ["cq", "bq0", "bq1"])
-        unpack(1)
-        if t > 0:
-            fcopy(0)
-            fcopy(1)
-        diag_k(0)
-        diag_k(1)
-        if t == 0:
-            quant_unit(2)
-            quant_unit(3)
-        unpack(2)
-        unpack(3)
-        scan(T.hb[:, 32:448], bank(7, CP), T.d1[:, CP:2 * CP], T.ini[:, 0:1], A.min, A.add,
-             ["#7", "d1a1", "d1b1", "d1c", "ini"], ["hb", "hb1"])
-        ts(T.key[:], T.dk[:, 15:C:16], c("offk"), None, A.subtract, None, ["dk0", "dk1", "offk"], ["key"])
-        scan(T.hb[:, 0:416], bank(6, CP), T.d1[:, 0:CP], T.ini[:, 1:2], A.min, A.add,
-             ["#6", "d1a0", "d1b0", "d1c", "ini"], ["hb"])
-        ts(T.keyf[:], T.key[:], -1.0, None, A.mult, None, ["key"], ["keyf"])
-        op("v", lambda: V.transpose(T.tab[:, 0:64], T.hb[:, 384:448]), ["hb", "hb1"], ["tab0"])
-        tt(T.fr[:], T.dk[:, 15:C:16], T.keyf[:], A.add, ["dk0", "dk1", "keyf"], ["fr"])
+        last = t + 1 == R
+        for b in range(4 if t else 1):
+            unpack(b)
+        op("v", lambda: V.transpose(T.tab[:, 0:64], T.hb[:, W:W + 64]), ["hb"], ["tab0"])
         act(T.tab[64:96, 64:128], T.tab[96:128, 0:64], AF.Copy, ["tab0"], ["tab1c"])
         act(T.tab[96:128, 64:128], T.tab[64:96, 0:64], AF.Copy, ["tab0"], ["tab1d"])
         cp(T.tab[0:32, 64:128], T.tab[32:64, 0:64], ["tab0"], ["tab1a"])
         cp(T.tab[32:64, 64:128], T.tab[0:32, 0:64], ["tab0"], ["tab1b"])
-
-        def classes(s):
-            ts(T.thr[:, s:120:5], T.fr[:], T.tg[:, s:s + 1], BIG, A.not_equal, A.mult, ["fr", "tg"], ["thr%d" % s])
-        classes(0)
-        classes(1)
+        if t == 0:
+            quant_unit(1)
         act(T.tab[64:128, 128:256], T.tab[0:64, 0:128], AF.Copy, ["tab0", "tab1a", "tab1b"], ["tab2b"])
         cp(T.tab[0:64, 128:256], T.tab[64:128, 0:128], ["tab0", "tab1c", "tab1d"], ["tab2a"])
-        classes(2)
         tab = ["tab0", "tab1a", "tab1b", "tab1c", "tab1d", "tab2a", "tab2b", "tabz", "key"]
         act(T.sn[:], T.tab[:, 0:512].indirect(T.key[:]), AF.Sign, tab, ["sn"], bias=-0.5, scale=-1.0)
-        for b in range(0 if t == 0 else 2, 4):
-            fcopy(b)
-        for b in range(4):
-            act(T.nf[:, C * b:C * b + C], T.ff[:, C * b:C * b + C], AF.Copy, ["ff%d" % b], ["nf%d" % b], scale=-1.0)
+        classes(2)
+        classes(3)
+        thr = ["thr%d" % s for s in range(5)]
         if t == 0:
             ts(T.ci[:], T.ik[:], c("r"), 0.2, A.add, A.mult, ["ik", "r"], ["ci"])
+        act(flags(1), T.thr[:], AF.Relu, thr + ["it1"], ["it1"], bias=1.0, scale=-1.0)
+        if t == 0:
+            act(T.inc[:, 4:120:5], T.idp[:], AF.Identity, ["idp", "r4"], ["inc4"], bias=c("r4"), scale=0.25)
         tt(T.mp[:], T.tab[:, 0:512].indirect(T.key[:]), T.jc[:], A.add, tab + ["jc"], ["mp"])
         if t == 0:
             ts(T.l2[:], T.ci[:], 23.0, 16.0, A.min, A.mult, ["ci"], ["l2"])
         scan(T.dm[:, 1:C + 1], T.d2[:], T.sn[:], 0.0, A.mult, A.add, ["d2", "sn"], ["dm"])
-        classes(3)
-        thr = ["thr%d" % s for s in range(4)]
-        tt(T.it[:, 1:512:4], T.dm[:, 16:C + 16].indirect(T.l2[:]), T.thr[:], A.is_gt, ["dm", "l2"] + thr, ["it"])
-        ranks(6, 7)
-        ts(T.pos[:], T.sm[:, 4:120:5], -float(DUMP), None, A.add, None, ["sm"], ["pos"])
+        if t == 0:
+            quant_unit(2)
+        tt(flags(0), T.dm[:, 16:C + 16].indirect(T.l2[:]), T.thr[:], A.is_gt, ["dm", "l2"] + thr, ["it0"])
+        if t == 0:
+            qz(const(3)[0], const(3)[1], T.cu[:], ["cu"], ["cq3"])
+        ranks(0, 6, 7)
+        ranks(1, 4, 5)
+        if t == 0:
+            quant_unit(3)
+            for b in range(1, 4):
+                unpack(b)
+        for b in range(4):
+            fcopy(b)
+        counts(7, range(4))
+        if t == 0:
+            ts(T.qi[:], c("r"), -1.5, 0.25, A.add, A.mult, ["r"], ["qi"])
+        within(6)
+        if t == 0:
+            cp(c("q4"), T.qi[:], ["qi"], ["q4"])
+            cs("el", T.qi[:], -4.0, c("r"), A.mult, A.add, ["qi", "r"])
+        choose()
+        if t == 0:
+            ts(T.d4[:], T.d4[:], c("q4"), -4608.0, A.is_equal, A.mult, ["d4", "q4"], ["d4"])
+            act(T.d4[:], T.d4[:], AF.Identity, ["d4"], ["d4"], bias=512.0, scale=1.0)
+            ca("b4", c("q4"), -512.0, 1536.0, ["q4"])
+            ca("b4", c("el"), -0.25, c("b4"), ["el", "b4"])
+        ts(T.pos[:], T.sm[:, 4:120:5], 4.0, -float(DUMP), A.mult, A.add, ["sm"], ["pos"])
         cp(T.win[:, 0:1984].indirect(T.pos[:]), T.mp[:], ["pos", "mp", "win"], ["win"])
-        scan(T.de[:], T.d0[:, 0:NS], T.win[:, SLOT0:SLOT0 + NS], 0.0, A.add, A.max, ["d0", "win"], ["de"])
-        ts(T.b16[:], T.de[:, 15:NS:16], c("boost"), None, A.subtract, None, ["de", "boost"], ["b16"])
-        ts(T.pi[:], T.de[:, 15:NS:16], 1024.0, None, A.mult, None, ["de"], ["pi"])
-        for b in range(4):
-            act(T.aa[:, NS * b:NS * b + NS], T.ff[:, C * b:C * b + C].indirect(T.b16[:]), AF.Copy,
-                ["ff%d" % b, "b16"], ["aa%d" % b])
-        ts(T.pb[:], T.pi[:], 1023, None, A.bitwise_and, None, ["pi"], ["pb"])
-        cp(T.a16[:], T.pb[:], ["pb"], ["a16"])
-        for b in range(4):
-            tt(T.ee[:, b:4 * NS:4], T.nf[:, C * b:C * b + C].indirect(T.a16[:]), T.aa[:, NS * b:NS * b + NS],
-               A.add, ["nf%d" % b, "a16", "aa%d" % b], ["ee%d" % b])
-        oq, oz, lq, lz = T["oq%d" % t], T["oz%d" % t], T["lq%d" % t], T["lz%d" % t]
-        sent = qz(oq[:], oz[:], T.ee[:], ["ee%d" % b for b in range(4)], ["oq%d" % t])
+        scan(T.de[:], T.d4[:], T.win[:, SLOT0:SLOT0 + NS], 0.0, A.add, A.max, ["d4", "win"], ["de"])
+        ts(T.b16[:], T.de[:, 3:NS:4], c("b4"), 4.0, A.subtract, A.mult, ["de", "b4"], ["b16"])
+        ts(T.pi[:], T.de[:, 3:NS:4], 16384.0, None, A.mult, None, ["de"], ["pi"])
+        nf = ["nf%d" % b for b in range(4)]
+        runs = ((0, 10), (10, 20), (20, 40))
+        for lo, hi in runs:
+            act(T.aa[:, 16 * lo:16 * hi], T.nf[:].indirect(T.b16[:, lo:hi]), AF.Copy, nf + ["b16"], ["aa%d" % lo],
+                scale=-1.0)
+        ts(T.pb[:], T.pi[:], 2047, None, A.bitwise_and, None, ["pi"], ["pb"])
+        ts(T.a16[:], T.pb[:], c("el"), None, A.add, None, ["pb", "el"], ["a16"])
         dst = T.cores[(rank + 1 + t) % N]
         rid, pid = topo.addr(dst)[0], topo.addr(dst)[1]
         mask = topo.mask(core, dst)
-        need("g", sent)
-        g.remote_dma(lq[:].bitcast(dt.uint8), oq[:].bitcast(dt.uint8), T.sem["arr%d" % t], T.sem.snt, pid, rid, mask)
-        g.remote_dma(lz[:], oz[:], T.sem["arr%d" % t], T.sem.snt, pid, rid, mask)
-        count["snt"] = count.get("snt", 0) + 2 * len(topo.engines(core, dst))
+        oq, oz, lq, lz = T["oq%d" % t], T["oz%d" % t], T["lq%d" % t], T["lz%d" % t]
+        arr, n = T.sem["arr%d" % t], NS // 2
+        for lo, hi in runs:
+            h = lo // 20
+            e = 512 * h + 16 * (lo - 20 * h)
+            tt(T.ee[:, e:e + 16 * (hi - lo)], T.nf[:].indirect(T.a16[:, lo:hi]), T.aa[:, 16 * lo:16 * hi], A.add,
+               nf + ["a16", "aa%d" % lo], ["ee%d" % lo])
+            if hi % 20:
+                continue
+            counts(5, (2 * h, 2 * h + 1))
+            o = 128 * h
+            need("g", qz(oq[:, o:o + 128], oz[:, o:o + 128], T.ee[:, 4 * o:4 * o + 512],
+                         ["ee%d" % a for a, b in runs if a // 20 == h] + ["ez%d" % h], []))
+            g.remote_dma(lq[:, n * h:n * h + n].bitcast(dt.uint8), oq[:, o:o + n].bitcast(dt.uint8), arr, T.sem.snt,
+                         pid, rid, mask)
+            g.remote_dma(lz[:, n * h:n * h + n], oz[:, o:o + n], arr, T.sem.snt, pid, rid, mask)
+        count["snt"] = count.get("snt", 0) + 4 * len(topo.engines(core, dst))
         src = T.cores[(rank - 1 - t) % N]
-        wrote["l%d" % t] = ("arr%d" % t, 2 * len(topo.engines(src, core)))
-        ts(T.it[:, 1:512:4], T.thr[:], 0.0, None, A.is_equal, None, thr, ["it"])
-        ranks(4, 5)
-        ts(T.tq[:], T.sm[:, 4:120:5], -2127.5, 1.0 / NS, A.add, A.mult, ["sm"], ["tq"])
-        ts(T.tr[:], T.tq[:], -float(NS), -2048.0, A.mult, A.add, ["tq"], ["tr"])
+        wrote["l%d" % t] = ("arr%d" % t, 4 * len(topo.engines(src, core)))
+        within(4)
+        choose()
+        ts(T.tq[:], T.sm[:, 4:120:5], -531.875, 4.0 / NS, A.add, A.mult, ["sm"], ["tq"])
+        ts(T.tr[:], T.tq[:], -NS / 4, -512.0, A.mult, A.add, ["tq"], ["tr"])
         tt(T.tv[:], T.tr[:], T.sm[:, 4:120:5], A.add, ["tr", "sm"], ["tv"])
-        cp(T.tk[:], T.tv[:], ["tv"], ["tk"])
-        if t + 1 < R:
-            ms(T.win[:, SLOT0:SLOT0 + NS], 0.0, ["win"])
-        if t == 0:
+        ts(T.tk[:], T.tv[:], 4.0, None, A.mult, None, ["tv"], ["tk"])
+        if last:
             qz(T.vq[:], T.vz[:], T.vb[:], ["vb"], ["vq"])
+        else:
+            fill(T.win[:, SLOT0:SLOT0 + NS], NS, 0.0, ["win"])
         for b in (0, 2, 1, 3):
             mm(4 + b, NS, unit(b)[0], unit(b)[1], lq[:], lz[:], ["eq%d" % b, "l%d" % t])
         for b in (0, 1):
             cp(T.gg[:, NS * b:NS * b + NS], bank(4 + b, NS), ["#%d" % (4 + b)], ["gg%d" % b])
         for b in (2, 3):
             act(T.gg[:, NS * b:NS * b + NS], bank(4 + b, NS), AF.Copy, ["#%d" % (4 + b)], ["gg%d" % b])
-        by_scalar = ((2, 3), (2, 3, 1))
-        for h in range(2):
-            for b in by_scalar[h]:
-                act(T.ga[:, C * b + H * h:C * b + H * h + H],
-                    T.gg[:, NS * b:NS * b + NS].indirect(T.tk[:, 12 * h:12 * h + 12]), AF.Copy,
-                    ["gg%d" % b, "tk"], ["ga%d_%d" % (h, b)])
-        last = t + 1 == R
 
-        def zadd(h, b):
-            out = T.zt[:, 4 * H * h + b:4 * H * h + 4 * H:4]
-            if b in by_scalar[h]:
-                tt(out, T.ps[:, 512 * b + H * h:512 * b + H * h + H], T.ga[:, C * b + H * h:C * b + H * h + H], A.add,
-                   ["#%d" % b, "ga%d_%d" % (h, b)], ["zt%d_%d" % (h, b)])
+        def taken(p, k):
+            return T.gg[:, NS * k:NS * k + NS].indirect(T.tk[:, 12 * p:12 * p + 12])
+
+        def gather(p):
+            for k in range(FUSED[p], 4):
+                act(cols(T.ga, 4 * p + k), taken(p, k), AF.Copy, ["gg%d" % k, "tk"], ["ga%d_%d" % (p, k)])
+
+        def zadd(p, k):
+            if k < FUSED[p]:
+                tt(plane(T.zt, p, k), taken(p, k), plane(T.nf, p, k), A.subtract,
+                   ["gg%d" % k, "tk", "nf%d" % k], ["zt%d_%d" % (p, k)])
             else:
-                tt(out, T.gg[:, NS * b:NS * b + NS].indirect(T.tk[:, 12 * h:12 * h + 12]),
-                   T.ff[:, C * b + H * h:C * b + H * h + H], A.add,
-                   ["gg%d" % b, "tk", "ff%d" % b], ["zt%d_%d" % (h, b)])
+                tt(plane(T.zt, p, k), bank(k, W, W * p), cols(T.ga, 4 * p + k), A.add,
+                   ["#%d" % k, "ga%d_%d" % (p, k)], ["zt%d_%d" % (p, k)])
 
-        def layer(h):
-            qz(cols(T.zq, h), cols(T.zz, h), T.zt[:, 4 * H * h:4 * H * h + 4 * H],
-               ["zt%d_%d" % (h, b) for b in range(4)], ["zq%d" % h])
-            for k in range(4):
-                bk = 4 * (1 - h) + k
-                mm(bk, H, T.wq[:, 128 * k:128 * k + 128], T.wz[:, 128 * k:128 * k + 128],
-                   cols(T.zq, h), cols(T.zz, h), ["wq", "wz", "zq%d" % h])
-                act(T.rr[:, C * k + H * h:C * k + H * h + H], bank(bk, H), AF.Relu, ["#%d" % bk], ["rr%d_%d" % (h, k)],
-                    scale=0.015625)
+        def layer(p):
+            qz(cols(T.zq, p), cols(T.zz, p), tile(T.zt, p), planes("zt", p), ["zq%d" % p])
+            for k in (0, 2, 1, 3):
+                mm(k + 4 * (p != 1), W, T.wq[:, 128 * k:128 * k + 128], T.wz[:, 128 * k:128 * k + 128],
+                   cols(T.zq, p), cols(T.zz, p), ["wq", "wz", "zq%d" % p])
 
-        def xadd(h, k):
-            tt(T.xs[:, 4 * H * h + k:4 * H * h + 4 * H:4], T.rr[:, C * k + H * h:C * k + H * h + H],
-               T.zt[:, 4 * H * h + k:4 * H * h + 4 * H:4], A.add,
-               ["rr%d_%d" % (h, k), "zt%d_%d" % (h, k)], ["xs%d_%d" % (h, k)])
+        def relu(p):
+            for k in (0, 2, 1, 3):
+                bk = k + 4 * (p != 1)
+                act(plane(T.rr, p, k), bank(bk, W), AF.Relu, ["#%d" % bk], ["rr%d_%d" % (p, k)], scale=0.015625)
 
-        def state(h):
-            quant_x(h, False)
+        def xadd(p, k):
+            lo, hi = 4 * W * p + k, 4 * W * p + 4 * W
+            zk = planes("zt", p)[k::2]
+            tt(T.zt[:, lo:hi:2], T.rr[:, lo:hi:2], T.zt[:, lo:hi:2], A.add, planes("rr", p)[k::2] + zk, zk)
+
+        def xdma(p):
+            op("g", lambda: g.dma_start(tile(T.zt, p), tile(T.rr, p), accum_op=A.add),
+               planes("rr", p), planes("zt", p), sem="gd", inc=16)
+
+        def state(p):
+            qz(cols(T.xq, p), cols(T.xz, p), tile(T.zt, p), planes("zt", p), ["xq%d" % p])
             if not last:
-                score(h)
-            else:
-                mm(4 + h, H, T.vq[:], T.vz[:], cols(T.xq, h), cols(T.xz, h), ["vq", "xq%d" % h])
-                dma("sy", "st_sy", T.oc[:, 4 * H * h:4 * H * h + 4 * H], cols(T.xq, h).bitcast(dt.uint8), ["xq%d" % h], [])
-        for b in range(4):
-            zadd(0, b)
-        zadd(1, 0)
-        layer(0)
-        for b in (2, 3, 1):
-            zadd(1, b)
-        xadd(0, 0)
-        layer(1)
-        for k in (1, 2, 3):
-            xadd(0, k)
-        xadd(1, 0)
-        state(0)
-        for k in (1, 2, 3):
-            xadd(1, k)
-        if not last:
-            signs(0)
-        state(1)
+                score(p)
+                return
+            b = score_bank[p]
+            mm(b, W, T.vq[:], T.vz[:], cols(T.xq, p), cols(T.xz, p), ["vq", "xq%d" % p])
+            dma("sy", "st_sy", tile(T.oc, p), cols(T.xq, p).bitcast(dt.uint8), ["xq%d" % p], [])
+            if "s%d" % p == LAST[-2:]:
+                for k in range(4):
+                    q, sem = (("a", "st_sc"), ("sy", "st_sy"))[k % 2]
+                    dma(q, sem, T.osc[4 * k:4 * k + 4, :], T.xz[32 * k:32 * k + 4, :], ["xq0", "xq1"], [])
+            act(cols(T.yy, p), bank(b, W), AF.Copy, ["#%d" % b], ["yy%d" % p])
+            dma("a", "st_sc", cols(T.y, p), cols(T.yy, p), ["yy%d" % p], [])
 
-    act(cols(T.yy, 0), bank(4, H), AF.Copy, ["#4"], ["yy0"])
-    dma("a", "st_sc", T.y[:, 0:H], cols(T.yy, 0), ["yy0"], [])
-    cp(cols(T.yy, 1), bank(5, H), ["#5"], ["yy1"])
-    for k in range(4):
-        q, sem = (("a", "st_sc"), ("sy", "st_sy"))[k % 2]
-        dma(q, sem, T.osc[4 * k:4 * k + 4, :], T.xz[32 * k:32 * k + 4, :], ["xq0", "xq1"], [])
-    dma("a", "st_sc", T.y[:, H:C], cols(T.yy, 1), ["yy1"], [])
+        whole = {"g": gather, "l": layer, "r": relu, "d": xdma, "s": state, **listing}
+        by_plane = {"z": zadd, "x": xadd}
+        for step in (LAST if last else ORDER).split():
+            if step[0] in whole:
+                whole[step[0]](int(step[1]))
+            else:
+                for k in step[3:]:
+                    by_plane[step[0]](int(step[1]), int(k))
+
     for s in ("v", "a", "p", "g", "snt", "st_sc", "st_sy"):
         need("sy", (s, count[s]))

from concourse.mybir import dt, AluOpType as A, AxisListType, ActivationFunctionType as AF

N, C, R, NS = 4, 384, 3, 160
W = C // 2
CP = C + 32
STEP = 1024.0
BIG = float(2 ** 30)
KW = 256.0
TINY = 1e-37
DUMP = 1600
SLOT0 = 2048 - DUMP
FUSED = (2, 1)
ORDER = ("g0 g1 z0.0123 z1.0 l0 r0 z1.123 l1 r1 x0.01 x1.0 s0 n0 x1.1 s1 q0 n1 k0 q1 a0 b0 k1 a1 f0 f1 b1 f2")
LAST = "g0 g1 z0.0123 z1.0 l0 r0 z1.123 l1 r1 x0.01 x1.0 s0 x1.1 s1"
F32, BF, I32, U16, CO, SC = "float32", "bfloat16", "int32", "uint16", "float8_e4m3fn_x4", "uint8"


def _s(n, d):
    return ("sbuf", [128, n], d)


SCRATCH = {
    "ps": ("psum", [128, 4096], F32),
    "x0": _s(4 * C, BF), "ub": _s(512, BF), "vb": _s(512, BF),
    "wq": _s(512, CO), "wz": _s(512, SC), "uq": _s(128, CO), "uz": _s(128, SC), "vq": _s(128, CO), "vz": _s(128, SC),
    "et": _s(528, BF), "eq": _s(512, CO), "ez": _s(512, SC),
    "ct": _s(516, BF), "cu": _s(512, BF), "cq": _s(512, CO), "cz": _s(512, SC),
    "xq": _s(C, CO), "xz": _s(C, SC),
    "zt": _s(4 * C, BF), "zq": _s(C, CO), "zz": _s(C, SC),
    "bt": _s(4 * (W + 32), BF), "bq": _s(CP, CO), "bz": _s(CP, SC),
    "it": _s(1024, BF), "iq": _s(256, CO), "iz": _s(256, SC),
    "nf": _s(4 * C, BF), "gg": _s(4 * NS, BF), "ga": _s(4 * C, BF), "aa": _s(4 * NS, BF),
    "ee": _s(1024, BF), "rr": _s(4 * C, F32), "yy": _s(C, F32),
    "ha": _s(2 * W, F32), "hb": _s(W + 64, F32), "tab": _s(512, F32), "dk": _s(C, F32), "mp": _s(C, F32),
    "dm": _s(C + 16, BF), "sn": _s(C, BF), "win": _s(1984, F32), "de": _s(NS, F32),
    "key": _s(24, U16), "keyf": _s(24, F32), "fr": _s(24, F32), "thr": _s(128, F32),
    "inc": _s(128, F32), "bb": _s(128, F32), "sm": _s(128, F32),
    "pos": _s(24, U16), "a16": _s(40, U16), "pi": _s(40, I32), "pb": _s(40, I32), "b16": _s(40, U16),
    "tq": _s(24, I32), "tr": _s(24, F32), "tv": _s(24, F32), "tk": _s(24, U16),
    "cs": _s(32, F32), "pv": _s(8, F32), "gi": _s(1, I32), "k4": _s(4, F32), "t8": _s(7, F32),
    "ko": _s(4, F32), "tg": _s(4, F32), "q2": _s(128, F32), "n2": _s(128, F32), "nb": _s(128, BF),
    "j16": _s(C, BF), "d0": _s(W, BF), "d2": _s(C, BF), "jc": _s(C, F32), "d1": _s(W + 32, BF),
    "ig": _s(128, F32), "d4": _s(NS, BF), "qi": _s(1, I32), "d1r": _s(120, F32),
    "big": _s(24, F32), "idp": _s(24, F32), "ik": _s(8, F32), "ci": _s(8, I32), "l2": _s(8, U16),
}
for _t in range(R):
    SCRATCH["oq%d" % _t] = _s(256, CO)
    SCRATCH["oz%d" % _t] = _s(256, SC)
    SCRATCH["lq%d" % _t] = _s(NS, CO)
    SCRATCH["lz%d" % _t] = _s(NS, SC)

SEMAPHORES = ["v", "a", "p", "g", "lx0", "lx1", "lu", "lv", "lwc", "lws", "arr0", "arr1", "arr2", "snt",
              "st_sy", "st_sc", "gd"]


def rank_program(g, core, T, topo):
    rank = T.rank_of(core)
    if rank is None:
        return
    Q = {"v": g.vector, "a": g.scalar, "p": g.tensor, "g": g, "sy": g.sync}
    known = {q: {} for q in Q}
    count = {}
    snap = {}
    wrote = {}
    read = {}

    def need(q, mark):
        sem, val = mark
        if known[q].get(sem, 0) >= val:
            return
        Q[q].wait_ge(T.sem[sem], val)
        for s, x in snap.get(mark, {}).items():
            if known[q].get(s, 0) < x:
                known[q][s] = x
        known[q][sem] = val

    def op(q, fn, rd, wr, sem=None, inc=1):
        sem = sem or q
        marks = {}

        def add(m, same):
            if m is None or (m[0] == q and (q == "p" or not same)):
                return
            if marks.get(m[0], 0) < m[1]:
                marks[m[0]] = m[1]
        for k in rd:
            add(wrote.get(k), True)
            if k[0] == "#":
                for m in read.get(k, []):
                    add(m, False)
        for k in wr:
            add(wrote.get(k), True)
            for m in read.get(k, []):
                add(m, True)
        for s in sorted(marks, key=lambda z: z == q):
            need(q, (s, marks[s]))
        count[sem] = count.get(sem, 0) + inc
        fn().then_inc(T.sem[sem], inc)
        mark = (sem, count[sem])
        snap[mark] = dict(known[q])
        for k in rd:
            read.setdefault(k, []).append(mark)
        for k in wr:
            wrote[k] = mark
            read[k] = []
        return mark

    V, S, P = g.vector, g.scalar, g.tensor

    def ts(out, in0, s1, s2, o0, o1, rd, wr):
        if o1 is None:
            return op("v", lambda: V.tensor_scalar(out, in0, s1, None, o0), rd, wr)
        return op("v", lambda: V.tensor_scalar(out, in0, s1, s2, o0, o1), rd, wr)

    def tt(out, in0, in1, o, rd, wr):
        return op("v", lambda: V.tensor_tensor(out, in0, in1, o), rd, wr)

    def cp(out, in_, rd, wr):
        return op("v", lambda: V.tensor_copy(out, in_), rd, wr)

    def ms(ap, val, wr):
        return op("v", lambda: V.memset(ap, val), [], wr)

    def scan(out, d0, d1, init, o0, o1, rd, wr):
        return op("v", lambda: V.tensor_tensor_scan(out, d0, d1, init, o0, o1), rd, wr)

    def qz(codes, scales, in_, rd, wr):
        return op("v", lambda: V.quantize_mx(codes, scales, in_), rd, wr)

    def act(out, in_, fn, rd, wr, bias=None, scale=None):
        if bias is None and scale is None:
            return op("a", lambda: S.activation(out, in_, fn), rd, wr)
        if bias is None:
            return op("a", lambda: S.activation(out, in_, fn, scale=scale), rd, wr)
        return op("a", lambda: S.activation(out, in_, fn, bias=bias, scale=scale), rd, wr)

    def bank(b, n, a=0):
        return T.ps[:, 512 * b + a:512 * b + a + n]

    def mm(b, n, lq, lz, rq, rz, rd):
        return op("p", lambda: P.matmul_mx(bank(b, n), lq, lz, rq, rz, True, True), rd, ["#%d" % b])

    def iota(out, pat, base, cm, wr):
        return op("g", lambda: g.iota(out, pat, base, cm, allow_small_or_imprecise_dtypes=True), [], wr)

    def asel(out, in_, pat, cmp, fill, base, cm, rd, wr):
        return op("g", lambda: g.affine_select(out, in_, pat, cmp, fill, base, cm), rd, wr)

    def dma(q, sem, out, in_, rd, wr):
        return op(q, lambda: Q[q].dma_start(out, in_), rd, wr, sem=sem, inc=16)

    names = ["r", "pw", "mg", "sg0", "sg", "w0", "w1", "f0", "k1", "c3", "r4", "a3", "own", "boost", "c8", "offk", "ofs",
             "q4", "el", "b4"]
    col = {n: i for i, n in enumerate(names)}

    def c(n):
        return T.cs[:, col[n]:col[n] + 1]

    def cs(n, in0, s1, s2, o0, o1, rd):
        return ts(c(n), in0, s1, s2, o0, o1, rd, [n])

    def ca(n, in_, scale, bias, rd):
        return act(c(n), in_, AF.Identity, rd, [n], bias=bias, scale=scale)

    def const(i):
        return T.cq[:, 128 * i:128 * i + 128], T.cz[:, 128 * i:128 * i + 128]

    def unit(b):
        return T.eq[:, 128 * b:128 * b + 128], T.ez[:, 128 * b:128 * b + 128]

    def cols(buf, p, n=W):
        return buf[:, W * p:W * p + n]

    def tile(buf, p):
        return buf[:, 4 * W * p:4 * W * p + 4 * W]

    def plane(buf, p, k):
        return buf[:, 4 * W * p + k:4 * W * p + 4 * W:4]

    def planes(name, p):
        return ["%s%d_%d" % (name, p, k) for k in range(4)]

    score_bank, key_bank, word_bank = (4, 0), (5, 1), ((6, 7), (3, 2))

    def score(p):
        b = score_bank[p]
        mm(b, W, T.uq[:], T.uz[:], cols(T.xq, p), cols(T.xz, p), ["uq", "xq%d" % p])

    def sign(p):
        b = score_bank[p]
        act(T.bt[:, 0:4 * W:4], bank(b, W), AF.Sign, ["#%d" % b, "btz"], ["bt"], bias=-TINY, scale=1.0)

    def signs(p, tail=0):
        n = W + tail
        qz(cols(T.bq, p, n), cols(T.bz, p, n), T.bt[:, 0:4 * n], ["bt"], ["bq%d" % p])
        mm(key_bank[p], W, const(2)[0], const(2)[1], cols(T.bq, p), cols(T.bz, p), ["cq2", "bq%d" % p])
        n = W + 32 * p
        for i in (1, 0):
            mm(word_bank[p][i], n, const(i)[0], const(i)[1], cols(T.bq, p, n), cols(T.bz, p, n), ["cq%d" % i, "bq%d" % p])

    def diag_k(p):
        b = key_bank[p]
        scan(cols(T.dk, p), T.d0[:, 0:W], bank(b, W), 0.0, A.add, A.max, ["d0", "#%d" % b], ["dk%d" % p])

    def words(p, i):
        b = word_bank[p][i]
        if p == 0:
            scan(cols(T.ha, i), bank(b, W), T.d1[:, 0:W], 0.0, A.min, A.add, ["#%d" % b, "d1"], ["ha%d" % i])
        else:
            scan(T.hb[:, 32 * i:32 * i + W + 32], bank(b, W + 32), T.d1[:], T.ha[:, W * i + W - 1:W * i + W],
                 A.min, A.add, ["#%d" % b, "d1", "ha%d" % i], ["hb"])

    def unpack(b):
        mm(b, C, unit(b)[0], unit(b)[1], T.xq[:], T.xz[:], ["eq%d" % b, "xq0", "xq1"])

    def fcopy(b):
        act(T.nf[:, b:4 * C:4], bank(b, C), AF.Copy, ["#%d" % b], ["nf%d" % b], scale=-1.0)

    def flags(i):
        return T.it[:, 512 * i + 3:512 * i + 512:4]

    def ranks(i, bu, bo):
        iq, iz = T.iq[:, 128 * i:128 * i + 128], T.iz[:, 128 * i:128 * i + 128]
        qz(iq, iz, T.it[:, 512 * i:512 * i + 512], ["it%d" % i], ["iq%d" % i])
        mm(bo, 128, const(0)[0], const(0)[1], iq, iz, ["cq0", "iq%d" % i])
        mm(bu, 128, const(3)[0], const(3)[1], iq, iz, ["cq3", "iq%d" % i])

    def counts(bo, classes):
        for s in classes:
            scan(T.inc[:, s:120:5], T.ps[:, 512 * bo + s:512 * bo + 120:5], T.big[:], s / 4 - 1.0, A.add, A.min,
                 ["#%d" % bo, "big"], ["inc%d" % s])

    def within(bu):
        tt(T.bb[:, 0:120], T.inc[:, 0:120], bank(bu, 120), A.subtract, ["inc%d" % s for s in range(5)] + ["#%d" % bu], ["bb"])

    def choose():
        scan(T.sm[:, 0:120], T.d1r[:], T.bb[:, 0:120], 0.0, A.add, A.max, ["d1r", "bb"], ["sm"])

    def fill(out, n, val, wr):
        act(out, T.et[:, 0:n], AF.Identity, ["et"], wr, bias=val, scale=0.0)

    def quant_unit(b):
        qz(unit(b)[0], unit(b)[1], T.et[:, 3 - b:515 - b], ["et"], ["eq%d" % b])

    dma("a", "lu", T.ub[:], T.u[:], [], ["ub"])
    dma("sy", "lx0", tile(T.x0, 0), tile(T.x, 0), [], ["x0_0"])
    dma("sy", "lx1", tile(T.x0, 1), tile(T.x, 1), [], ["x0_1"])
    dma("sy", "lwc", T.wq[:].bitcast(dt.uint8), T.wc[:], ["x0_1"], ["wq"])
    dma("sy", "lws", T.wz[:], T.ws[:], [], ["wz"])
    dma("sy", "lv", T.vb[:], T.v[:], [], ["vb"])

    pf = T.pv[:, 0:1]
    iota(T.pv[:], [[-16, 8]], 0, 1, ["pv"])
    iota(T.q2[:], [[128, 4], [2, 32]], 1, 0, ["q2"])
    iota(T.ig[:], [[16, 8], [0, 16]], 0, -1, ["ig"])
    iota(T.j16[:], [[0, 24], [1, 16]], 0, 0, ["j16"])
    ms(T.et[:], 0.0, ["et"])
    fill(T.bt[:, 0:512], 512, 0.0, ["btz0"])
    fill(T.bt[:, 512:896], 384, 0.0, ["btz"])
    ts(T.t8[:], T.pv[:, 1:8], 0.0, 1.0, A.is_ge, A.add, ["pv"], ["t8"])
    ts(T.gi[:], pf, -7.5, 1.0 / 16, A.add, A.mult, ["pv"], ["gi"])
    op("v", lambda: V.tensor_reduce(c("pw"), T.t8[:], AxisListType.X, A.mult), ["t8"], ["pw"])
    cs("r", T.gi[:], -16.0, pf, A.mult, A.add, ["gi", "pv"])
    cs("mg", c("pw"), 6.0 * 2 ** 23, None, A.mult, None, ["pw"])
    cs("sg0", c("pw"), 64.0, -1.0, A.is_ge, A.mult, ["pw"])
    ts(T.n2[:], T.q2[:], c("mg"), c("mg"), A.add, A.subtract, ["q2", "mg"], ["n2"])
    cs("sg", c("sg0"), 0.5, c("pw"), A.add, A.mult, ["sg0", "pw"])
    tt(T.n2[:], T.q2[:], T.n2[:], A.subtract, ["q2", "n2"], ["n2"])
    cs("w0", c("r"), 0.0, KW, A.is_equal, A.mult, ["r"])
    act(T.nb[:], T.n2[:], AF.Sign, ["n2"], ["nb"])
    cs("f0", c("pw"), 32.0, -2.0, A.is_equal, A.mult, ["pw"])
    cs("k1", c("r"), 0.0, c("pw"), A.is_equal, A.mult, ["r", "pw"])
    cs("w1", c("f0"), 1.0, c("w0"), A.add, A.mult, ["f0", "w0"])
    ts(T.ct[:, 3:512:4], T.ig[:], c("r"), 0.0, A.add, A.is_equal, ["ig", "r"], ["ct3"])
    act(c("c3"), c("r"), AF.Relu, ["r"], ["c3"], bias=3.0 / 16, scale=-1.0 / 16)
    cs("a3", c("sg"), -1.0 / KW, (128.0 - 3.0 / 16) / KW, A.mult, A.add, ["sg"])
    ts(T.ko[:], T.nb[:, 0:128:32], c("k1"), 0.5, A.mult, A.mult, ["nb", "k1"], ["ko"])
    cs("own", c("a3"), c("w0"), c("c3"), A.mult, A.add, ["a3", "w0", "c3"])
    for i in range(2):
        act(T.ct[:, i:512:4], T.nb[:], AF.Identity, ["nb", "w%d" % i], ["ct%d" % i], bias=0.0, scale=c("w%d" % i))
    ms(T.ct[:, 512:516], 0.0, ["ct4"])
    for a in range(4):
        ts(T.ct[:, 128 * a + 2:128 * a + 128:4], T.ct[:, 128 * a + 3:128 * a + 128:4], c("own"), T.ko[:, a:a + 1],
           A.mult, A.add, ["ct3", "own", "ko"], ["ct2_%d" % a])
    fill(T.d1[:, 0:W], W, -1.0, ["d1a"])
    fill(T.d1[:, W + 1:W + 32], 31, 0.0, ["d1b"])
    fill(T.d1[:, W:W + 1], 1, 8 * KW, ["d1"])
    qz(T.uq[:], T.uz[:], T.ub[:], ["ub"], ["uq"])
    iota(T.k4[:], [[1, 4]], 0, 0, ["k4"])
    iota(T.jc[:], [[1, C]], 0, 0, ["jc"])
    iota(T.tab[:, 256:512], [[0, 256]], 0, 0, ["tabz"])
    asel(T.et[:, 3:515:4], T.et[:, 3:515:4], [[-1, 128]], A.not_equal, 1.0, 0, 1, ["et"], ["et"])
    iota(T.cu[:], [[0, 512]], 0, 0, ["cu"])

    cts = ["ct0", "ct1", "ct3", "ct4"] + ["ct2_%d" % a for a in range(4)]
    qz(cols(T.xq, 0), cols(T.xz, 0), tile(T.x0, 0), ["x0_0"], ["xq0"])
    score(0)
    sign(0)
    ts(T.d2[:], T.j16[:], c("r"), 2.0, A.not_equal, A.mult, ["j16", "r"], ["d2"])
    for i in (2, 1, 0):
        qz(const(i)[0], const(i)[1], T.ct[:, i:i + 512], cts, ["cq%d" % i])
    act(T.d0[:], T.d2[:, 0:W], AF.Identity, ["d2"], ["d0"], bias=-31 * STEP, scale=16 * STEP)
    act(T.jc[:], T.jc[:], AF.Identity, ["jc"], ["jc"], bias=float(C), scale=1.0 / 4096)
    qz(cols(T.xq, 1), cols(T.xz, 1), tile(T.x0, 1), ["x0_1"], ["xq1"])
    score(1)
    signs(0)
    sign(1)
    ca("boost", c("r"), -STEP, 15.0 * STEP, ["r"])
    ca("c8", c("sg"), -1.0, -255.6875, ["sg"])
    ca("r4", c("r"), 0.25, 0.0, ["r"])
    ca("offk", c("c8"), 1.0, c("boost"), ["c8", "boost"])
    ca("ofs", c("offk"), -BIG, 0.0, ["offk"])
    act(T.tg[:], T.k4[:], AF.Identity, ["k4", "ofs"], ["tg"], bias=c("ofs"), scale=-BIG / 8)
    fill(T.it[:, 512:1024], 512, 0.0, ["it1"])
    asel(T.cu[:, 3:512:4], T.ct[:, 3:512:4], [[-1, 128]], A.is_ge, 0.0, 0, 1, ["ct3", "cu"], ["cu"])
    asel(T.cu[:, 3:512:4], T.cu[:, 3:512:4], [[-1, 128]], A.not_equal, -512.0, 0, 1, ["cu"], ["cu"])
    iota(T.ik[:], [[16, 8]], -2, 0, ["ik"])
    iota(T.thr[:, 4:128:5], [[0, 25]], 1000000, 0, ["thr4"])
    iota(T.thr[:, 120:128], [[0, 8]], 1000000, 0, ["thr4"])
    iota(T.it[:, 0:512], [[0, 512]], 0, 0, ["it0"])
    iota(T.big[:], [[0, 24]], 1000000, 0, ["big"])
    iota(T.idp[:], [[16, 24]], DUMP, 0, ["idp"])
    iota(T.d1r[:], [[0, 120]], 0, 0, ["d1r"])
    iota(T.d1r[:, 0:120:5], [[0, 24]], -1000000, 0, ["d1r"])
    iota(T.win[:, SLOT0:SLOT0 + NS], [[0, NS]], 0, 0, ["win"])
    iota(T.d4[:], [[0, NS // 4], [1, 4]], 0, 0, ["d4"])
    for h in range(2):
        iota(T.ee[:, 512 * h + 2 * NS:512 * h + 512], [[0, 512 - 2 * NS]], 0, 0, ["ez%d" % h])

    def classes(s):
        act(T.thr[:, s:120:5], T.fr[:], AF.Abs, ["fr", "tg"], ["thr%d" % s], bias=T.tg[:, s:s + 1], scale=BIG)

    def split(i):
        dks = ["dk0", "dk1"]
        if i == 0:
            ts(T.key[:], T.dk[:, 15:C:16], c("offk"), None, A.subtract, None, dks + ["offk"], ["key"])
        elif i == 1:
            ts(T.keyf[:], T.key[:], -1.0, None, A.mult, None, ["key"], ["keyf"])
        else:
            tt(T.fr[:], T.dk[:, 15:C:16], T.keyf[:], A.add, dks + ["keyf"], ["fr"])
            classes(0)
            classes(1)
    listing = {"n": sign, "q": signs, "k": diag_k, "a": lambda p: words(p, 1), "b": lambda p: words(p, 0), "f": split}
    quant_unit(0)
    diag_k(0)
    signs(1, 32)
    for step in "a0 b0 k1 a1 f0 f1 b1 f2".split():
        listing[step[0]](int(step[1]))

    for t in range(R):
        last = t + 1 == R
        for b in range(4 if t else 1):
            unpack(b)
        op("v", lambda: V.transpose(T.tab[:, 0:64], T.hb[:, W:W + 64]), ["hb"], ["tab0"])
        act(T.tab[64:96, 64:128], T.tab[96:128, 0:64], AF.Copy, ["tab0"], ["tab1c"])
        act(T.tab[96:128, 64:128], T.tab[64:96, 0:64], AF.Copy, ["tab0"], ["tab1d"])
        cp(T.tab[0:32, 64:128], T.tab[32:64, 0:64], ["tab0"], ["tab1a"])
        cp(T.tab[32:64, 64:128], T.tab[0:32, 0:64], ["tab0"], ["tab1b"])
        if t == 0:
            quant_unit(1)
        act(T.tab[64:128, 128:256], T.tab[0:64, 0:128], AF.Copy, ["tab0", "tab1a", "tab1b"], ["tab2b"])
        cp(T.tab[0:64, 128:256], T.tab[64:128, 0:128], ["tab0", "tab1c", "tab1d"], ["tab2a"])
        tab = ["tab0", "tab1a", "tab1b", "tab1c", "tab1d", "tab2a", "tab2b", "tabz", "key"]
        act(T.sn[:], T.tab[:, 0:512].indirect(T.key[:]), AF.Sign, tab, ["sn"], bias=-0.5, scale=-1.0)
        classes(2)
        classes(3)
        thr = ["thr%d" % s for s in range(5)]
        if t == 0:
            ts(T.ci[:], T.ik[:], c("r"), 0.2, A.add, A.mult, ["ik", "r"], ["ci"])
        act(flags(1), T.thr[:], AF.Relu, thr + ["it1"], ["it1"], bias=1.0, scale=-1.0)
        if t == 0:
            act(T.inc[:, 4:120:5], T.idp[:], AF.Identity, ["idp", "r4"], ["inc4"], bias=c("r4"), scale=0.25)
        tt(T.mp[:], T.tab[:, 0:512].indirect(T.key[:]), T.jc[:], A.add, tab + ["jc"], ["mp"])
        if t == 0:
            ts(T.l2[:], T.ci[:], 23.0, 16.0, A.min, A.mult, ["ci"], ["l2"])
        scan(T.dm[:, 1:C + 1], T.d2[:], T.sn[:], 0.0, A.mult, A.add, ["d2", "sn"], ["dm"])
        if t == 0:
            quant_unit(2)
        tt(flags(0), T.dm[:, 16:C + 16].indirect(T.l2[:]), T.thr[:], A.is_gt, ["dm", "l2"] + thr, ["it0"])
        if t == 0:
            qz(const(3)[0], const(3)[1], T.cu[:], ["cu"], ["cq3"])
        ranks(0, 6, 7)
        ranks(1, 4, 5)
        if t == 0:
            quant_unit(3)
            for b in range(1, 4):
                unpack(b)
        for b in range(4):
            fcopy(b)
        counts(7, range(4))
        if t == 0:
            ts(T.qi[:], c("r"), -1.5, 0.25, A.add, A.mult, ["r"], ["qi"])
        within(6)
        if t == 0:
            cp(c("q4"), T.qi[:], ["qi"], ["q4"])
            cs("el", T.qi[:], -4.0, c("r"), A.mult, A.add, ["qi", "r"])
        choose()
        if t == 0:
            ts(T.d4[:], T.d4[:], c("q4"), -4608.0, A.is_equal, A.mult, ["d4", "q4"], ["d4"])
            act(T.d4[:], T.d4[:], AF.Identity, ["d4"], ["d4"], bias=512.0, scale=1.0)
            ca("b4", c("q4"), -512.0, 1536.0, ["q4"])
            ca("b4", c("el"), -0.25, c("b4"), ["el", "b4"])
        ts(T.pos[:], T.sm[:, 4:120:5], 4.0, -float(DUMP), A.mult, A.add, ["sm"], ["pos"])
        cp(T.win[:, 0:1984].indirect(T.pos[:]), T.mp[:], ["pos", "mp", "win"], ["win"])
        scan(T.de[:], T.d4[:], T.win[:, SLOT0:SLOT0 + NS], 0.0, A.add, A.max, ["d4", "win"], ["de"])
        ts(T.b16[:], T.de[:, 3:NS:4], c("b4"), 4.0, A.subtract, A.mult, ["de", "b4"], ["b16"])
        ts(T.pi[:], T.de[:, 3:NS:4], 16384.0, None, A.mult, None, ["de"], ["pi"])
        nf = ["nf%d" % b for b in range(4)]
        runs = ((0, 10), (10, 20), (20, 40))
        for lo, hi in runs:
            act(T.aa[:, 16 * lo:16 * hi], T.nf[:].indirect(T.b16[:, lo:hi]), AF.Copy, nf + ["b16"], ["aa%d" % lo],
                scale=-1.0)
        ts(T.pb[:], T.pi[:], 2047, None, A.bitwise_and, None, ["pi"], ["pb"])
        ts(T.a16[:], T.pb[:], c("el"), None, A.add, None, ["pb", "el"], ["a16"])
        dst = T.cores[(rank + 1 + t) % N]
        rid, pid = topo.addr(dst)[0], topo.addr(dst)[1]
        mask = topo.mask(core, dst)
        oq, oz, lq, lz = T["oq%d" % t], T["oz%d" % t], T["lq%d" % t], T["lz%d" % t]
        arr, n = T.sem["arr%d" % t], NS // 2
        for lo, hi in runs:
            h = lo // 20
            e = 512 * h + 16 * (lo - 20 * h)
            tt(T.ee[:, e:e + 16 * (hi - lo)], T.nf[:].indirect(T.a16[:, lo:hi]), T.aa[:, 16 * lo:16 * hi], A.add,
               nf + ["a16", "aa%d" % lo], ["ee%d" % lo])
            if hi % 20:
                continue
            counts(5, (2 * h, 2 * h + 1))
            o = 128 * h
            need("g", qz(oq[:, o:o + 128], oz[:, o:o + 128], T.ee[:, 4 * o:4 * o + 512],
                         ["ee%d" % a for a, b in runs if a // 20 == h] + ["ez%d" % h], []))
            g.remote_dma(lq[:, n * h:n * h + n].bitcast(dt.uint8), oq[:, o:o + n].bitcast(dt.uint8), arr, T.sem.snt,
                         pid, rid, mask)
            g.remote_dma(lz[:, n * h:n * h + n], oz[:, o:o + n], arr, T.sem.snt, pid, rid, mask)
        count["snt"] = count.get("snt", 0) + 4 * len(topo.engines(core, dst))
        src = T.cores[(rank - 1 - t) % N]
        wrote["l%d" % t] = ("arr%d" % t, 4 * len(topo.engines(src, core)))
        within(4)
        choose()
        ts(T.tq[:], T.sm[:, 4:120:5], -531.875, 4.0 / NS, A.add, A.mult, ["sm"], ["tq"])
        ts(T.tr[:], T.tq[:], -NS / 4, -512.0, A.mult, A.add, ["tq"], ["tr"])
        tt(T.tv[:], T.tr[:], T.sm[:, 4:120:5], A.add, ["tr", "sm"], ["tv"])
        ts(T.tk[:], T.tv[:], 4.0, None, A.mult, None, ["tv"], ["tk"])
        if last:
            qz(T.vq[:], T.vz[:], T.vb[:], ["vb"], ["vq"])
        else:
            fill(T.win[:, SLOT0:SLOT0 + NS], NS, 0.0, ["win"])
        for b in (0, 2, 1, 3):
            mm(4 + b, NS, unit(b)[0], unit(b)[1], lq[:], lz[:], ["eq%d" % b, "l%d" % t])
        for b in (0, 1):
            cp(T.gg[:, NS * b:NS * b + NS], bank(4 + b, NS), ["#%d" % (4 + b)], ["gg%d" % b])
        for b in (2, 3):
            act(T.gg[:, NS * b:NS * b + NS], bank(4 + b, NS), AF.Copy, ["#%d" % (4 + b)], ["gg%d" % b])

        def taken(p, k):
            return T.gg[:, NS * k:NS * k + NS].indirect(T.tk[:, 12 * p:12 * p + 12])

        def gather(p):
            for k in range(FUSED[p], 4):
                act(cols(T.ga, 4 * p + k), taken(p, k), AF.Copy, ["gg%d" % k, "tk"], ["ga%d_%d" % (p, k)])

        def zadd(p, k):
            if k < FUSED[p]:
                tt(plane(T.zt, p, k), taken(p, k), plane(T.nf, p, k), A.subtract,
                   ["gg%d" % k, "tk", "nf%d" % k], ["zt%d_%d" % (p, k)])
            else:
                tt(plane(T.zt, p, k), bank(k, W, W * p), cols(T.ga, 4 * p + k), A.add,
                   ["#%d" % k, "ga%d_%d" % (p, k)], ["zt%d_%d" % (p, k)])

        def layer(p):
            qz(cols(T.zq, p), cols(T.zz, p), tile(T.zt, p), planes("zt", p), ["zq%d" % p])
            for k in (0, 2, 1, 3):
                mm(k + 4 * (p != 1), W, T.wq[:, 128 * k:128 * k + 128], T.wz[:, 128 * k:128 * k + 128],
                   cols(T.zq, p), cols(T.zz, p), ["wq", "wz", "zq%d" % p])

        def relu(p):
            for k in (0, 2, 1, 3):
                bk = k + 4 * (p != 1)
                act(plane(T.rr, p, k), bank(bk, W), AF.Relu, ["#%d" % bk], ["rr%d_%d" % (p, k)], scale=0.015625)

        def xadd(p, k):
            lo, hi = 4 * W * p + k, 4 * W * p + 4 * W
            zk = planes("zt", p)[k::2]
            tt(T.zt[:, lo:hi:2], T.rr[:, lo:hi:2], T.zt[:, lo:hi:2], A.add, planes("rr", p)[k::2] + zk, zk)

        def xdma(p):
            op("g", lambda: g.dma_start(tile(T.zt, p), tile(T.rr, p), accum_op=A.add),
               planes("rr", p), planes("zt", p), sem="gd", inc=16)

        def state(p):
            qz(cols(T.xq, p), cols(T.xz, p), tile(T.zt, p), planes("zt", p), ["xq%d" % p])
            if not last:
                score(p)
                return
            b = score_bank[p]
            mm(b, W, T.vq[:], T.vz[:], cols(T.xq, p), cols(T.xz, p), ["vq", "xq%d" % p])
            dma("sy", "st_sy", tile(T.oc, p), cols(T.xq, p).bitcast(dt.uint8), ["xq%d" % p], [])
            if "s%d" % p == LAST[-2:]:
                for k in range(4):
                    q, sem = (("a", "st_sc"), ("sy", "st_sy"))[k % 2]
                    dma(q, sem, T.osc[4 * k:4 * k + 4, :], T.xz[32 * k:32 * k + 4, :], ["xq0", "xq1"], [])
            act(cols(T.yy, p), bank(b, W), AF.Copy, ["#%d" % b], ["yy%d" % p])
            dma("a", "st_sc", cols(T.y, p), cols(T.yy, p), ["yy%d" % p], [])

        whole = {"g": gather, "l": layer, "r": relu, "d": xdma, "s": state, **listing}
        by_plane = {"z": zadd, "x": xadd}
        for step in (LAST if last else ORDER).split():
            if step[0] in whole:
                whole[step[0]](int(step[1]))
            else:
                for k in step[3:]:
                    by_plane[step[0]](int(step[1]), int(k))

    for s in ("v", "a", "p", "g", "snt", "st_sc", "st_sy"):
        need("sy", (s, count[s]))
